import numpy as np, ml_dtypes
CORES = [48,51,52,55]
N = 4
import mx_ref
BF = ml_dtypes.bfloat16
def cols(t, e):
    v = np.concatenate([t.reshape(128, -1, 4), np.zeros((128, 1, 4), BF)], axis=1)
    return np.ascontiguousarray(v[:, e]).reshape(128, -1)
def cut(t, i, w=512):
    return t[:, w * i:w * i + w]
def pick(q, e):
    c = np.concatenate([q[0].reshape(128, -1, 4), np.zeros((128, 1, 4), np.uint8)], axis=1); s = np.concatenate([q[1], np.ones((16, 1), np.uint8)], axis=1)
    return (np.ascontiguousarray(c[:, e].reshape(128, -1)), np.ascontiguousarray(s[:, e]))
def join(*qs):
    return (np.concatenate([q[0] for q in qs], axis=1), np.concatenate([q[1] for q in qs], axis=1))
def put(q, e, v):
    c, s = q[0].reshape(128, -1, 4).copy(), q[1].copy(); c[:, e] = v[0].reshape(128, -1, 4); s[:, e] = v[1]
    return (c.reshape(128, -1), s)
def pk(c, s):
    return (np.ascontiguousarray(c), mx_ref.live(s))
def emit(q):
    return q[0], q[1]
def decode(q):
    o = []
    for b in range(4):
        e = np.zeros((128, 128, 4), np.float32); e[np.arange(128), np.arange(128), b] = 1
        o.append(mx_ref.matmul(mx_ref.quantize(e.reshape(128, 512).astype(BF)), q))
    return np.stack(o, axis=2).reshape(128, -1)
def f(rng, *shape):
    return mx_ref.flush((rng.standard_normal(shape, dtype=np.float32) * np.exp2(rng.integers(-2, 3, shape[:-1] + (1,)))).astype(BF))
def wide(rng, *shape, cols=0):
    v = rng.standard_normal(shape, dtype=np.float32) * np.exp2(rng.integers(-12, 13, shape)).astype(np.float32)
    if cols: v *= np.repeat(np.exp2(rng.integers(-cols, cols + 1, shape[:-2] + (1, shape[-1] // 4))) * (rng.random(shape[:-2] + (1, shape[-1] // 4)) > 0.0625), 4, axis=-1).astype(np.float32)
    return mx_ref.flush(v.astype(BF))
T, C = 384, 96
def best(s):
    return np.argsort(-(s + np.float32(0)), kind="stable")[:C]
def quant(u, v):
    qu = [mx_ref.quantize(np.ascontiguousarray(u[r])) for r in range(N)]
    return qu, [[mx_ref.quantize(np.ascontiguousarray(cut(v[r], i))) for i in range(4)] for r in range(N)]
def layer(q, qu, qv):
    e = best(mx_ref.matmul(qu, q)[0])
    old = pick(q, e)
    a = np.stack([mx_ref.matmul(t, old) for t in qv], axis=2)
    new = np.maximum(a, np.float32(0)) * np.float32(0.05) + decode(old).reshape(128, C, 4)
    return e, new.reshape(128, -1).astype(BF)
def setup_inputs(rng):
    u = np.zeros((N, 128, 512), BF)
    u[:, :, :4] = f(rng, N, 128, 4)
    return {"x": f(rng, N, 128, 4 * T), "u": u, "v": f(rng, N, 128, 2048), "w": f(rng, N, 128, 512)}
def setup_inputs_spread(rng):
    d = setup_inputs(rng)
    d["x"] = wide(rng, N, 128, 4 * T, cols=3)
    return d
def setup_inputs_ties(rng):
    d = setup_inputs(rng)
    d["x"] = np.stack([cols(d["x"][r], rng.permutation(T) % 5 - 1) for r in range(N)])
    d["u"][1::2] = 0
    return d
def setup_inputs_again(rng):
    d = setup_inputs(rng)
    x, u = d["x"].astype(np.float32).reshape(N, 128, T, 4), np.zeros((N, 128, 512), np.float32)
    good = np.stack([rng.permutation(T) < C for r in range(N)])
    x[:, :32] = (1 + rng.random((N, 32, T, 4))) * np.where(good, 1.0, -1.0)[:, None, :, None]
    u[:, :32, :4] = 1 + rng.random((N, 32, 4))
    d["x"], d["u"] = x.reshape(N, 128, 4 * T).astype(BF), u.astype(BF)
    return d
def setup_inputs_other(rng):
    d = setup_inputs(rng)
    x, u = d["x"].astype(np.float32).reshape(N, 128, T, 4), np.zeros((N, 128, 512), np.float32)
    v = d["v"].astype(np.float32).reshape(N, 128, 4, 128, 4)
    large = np.stack([rng.permutation(T) < C for r in range(N)])
    x[:, :16] = (1 + rng.random((N, 16, T, 4))) * np.where(large, 16.0, 1.0)[:, None, :, None]
    x[:, 16:32] = (0.25 + 0.25 * rng.random((N, 16, T, 4))) * rng.choice([-1.0, 1.0], (N, 16, T, 4))
    u[:, :16, :4] = 1 + rng.random((N, 16, 4))
    u[:, 16:32, :4] = -1 - rng.random((N, 16, 4))
    v[:, :, :, 16:32] = 0
    v[:, :16, :, 16:32] = 256 * (1 + rng.random((N, 16, 4, 16, 4)))
    d["x"], d["u"], d["v"] = x.reshape(N, 128, 4 * T).astype(BF), u.astype(BF), v.reshape(N, 128, 2048).astype(BF)
    return d
def setup_inputs_neg(rng):
    d = setup_inputs(rng)
    d["x"] = np.abs(d["x"].astype(np.float32)).astype(BF)
    d["v"] = (-np.abs(d["v"].astype(np.float32))).astype(BF)
    return d
def check_inputs(d):
    b = []
    for k in ("x", "u", "v", "w"):
        a = np.abs(d[k].astype(np.float32))
        if not (np.isfinite(a).all() and ((a == 0) | (a >= 2.0 ** -30) & (a <= 2.0 ** 30)).all()): b.append("a value of " + k)
    if (d["u"][:, :, 4:].astype(np.float32) != 0).any(): b.append("u has numbers behind its column 0")
    if b: return b
    qu, qv = quant(d["u"], d["v"])
    for r in range(N):
        q = mx_ref.quantize(np.ascontiguousarray(d["x"][r]))
        for k in (1, 2):
            e, new = layer(q, qu[(r + k) % N], qv[(r + k) % N])
            a = np.abs(new.astype(np.float32)).reshape(16, 8, C, 4).max(axis=(1, 3))
            if not ((a == 0) | (a >= 2.0 ** -30) & (a <= 2.0 ** 30)).all(): return ["a number of a made column"]
            q = put(q, e, mx_ref.quantize(new))
    return b
def reference(x, u, v, w):
    oc, osc = np.zeros((N, 128, 4 * T), np.uint8), np.zeros((N, 16, T), np.uint8)
    li, y = np.zeros((N, 2, C), np.float32), np.zeros((N, 128, T), np.float32)
    qu, qv = quant(u, v)
    for d in range(N):
        r = (d - 2) % N
        q = mx_ref.quantize(np.ascontiguousarray(x[r]))
        for k in (1, 2):
            s = (r + k) % N
            e, new = layer(q, qu[s], qv[s])
            q = put(q, e, mx_ref.quantize(new))
            li[d, k - 1] = e
        oc[d], osc[d] = emit(q)
        y[d] = mx_ref.matmul(mx_ref.quantize(np.ascontiguousarray(w[d])), q)
    return {"oc": oc, "osc": osc, "li": li, "y": y}

@@ -1,0 +1,445 @@
+import numpy as np
+from concourse.bass import DstId, RemoteDMATransfer
+from concourse.mybir import dt, AluOpType, AxisListType, ActivationFunctionType
+
+F8 = "float8_e4m3fn_x4"
+CH = 96
+NT = 384
+HALF = CH + NT
+T0 = HALF + CH
+
+
+def sb(n, d):
+    return ("sbuf", [128, n], d)
+
+
+def codes(**names):
+    d = {}
+    for k, n in names.items():
+        d[k], d[k + "s"] = sb(n, F8), sb(n, "uint8")
+    return d
+
+
+SCRATCH = {
+    "ps": ("psum", [128, 4096], "float32"),
+    "ub": sb(512, "bfloat16"), "xb": sb(4 * NT, "bfloat16"), "vb": sb(2048, "bfloat16"), "wb": sb(512, "bfloat16"),
+    "ones": sb(128, "bfloat16"), "zero": sb(512, "bfloat16"), "z16": sb(8, "uint16"), "eb": sb(520, "bfloat16"),
+    "tri": sb(128, "bfloat16"), "q0": sb(128, "bfloat16"), "qm": sb(128, "bfloat16"), "pp": sb(128, "bfloat16"),
+    "kc": sb(48, "float32"), "jj": sb(96, "int32"), "kk": sb(96, "int32"), "j16": sb(96, "int32"),
+    "ja": sb(96, "int32"), "jb": sb(96, "int32"), "jk": sb(96, "int32"), "g3": sb(16, "int32"), "g3a": sb(16, "int32"),
+    "g3b": sb(16, "int32"), "i3": sb(16, "int32"), "p16": sb(4, "int32"), "p128": sb(4, "int32"),
+    "p16f": sb(4, "float32"), "s4": sb(4, "float32"), "ab": sb(48, "float32"), "ab2": sb(8, "float32"),
+    "mk1": sb(16, "bfloat16"), "mk2": sb(96, "float32"), "thr": sb(96, "float32"),
+    "w1b": sb(512, "bfloat16"), "w2b": sb(512, "bfloat16"), "zb": sb(768, "bfloat16"),
+    "sc": sb(3, "float32"), "dl": sb(3, "float32"), "mt": sb(NT, "float32"), "cmp": sb(4 * NT, "bfloat16"),
+    "kl": sb(52, "float32"), "x0": sb(48, "float32"), "wx": sb(560, "bfloat16"),
+    "sel": sb(8, "float32"), "rkp": sb(4, "float32"), "hl": sb(8, "float32"), "hm": sb(8, "float32"), "hn": sb(8, "float32"),
+    "xo": sb(512, "bfloat16"), "xo2": sb(512, "bfloat16"),
+    "lst1": sb(6, "uint16"), "offc": sb(3, "uint16"), "off2f": sb(24, "float32"), "off2": sb(24, "uint16"),
+    "lin": sb(6, "uint16"), "offd": ("dram", [128, 3], "uint16"), "off1": sb(24, "uint16"), "off1f": sb(24, "float32"),
+    "hrb": sb(4 * CH, "float32"), "hr0": sb(4 * NT, "float32"), "hr1": sb(4 * CH, "float32"),
+    "hb": sb(512, "bfloat16"), "hx": sb(4 * HALF, "bfloat16"),
+    "yb": sb(NT, "float32"), "yw": sb(2 * HALF, "float32"), "lif": sb(12, "float32"),
+}
+SCRATCH.update(codes(uq=128, ur1=128, ur2=128, t0=NT, vq=512, wq=128, eq=512, w1=128, w2=128, zq=192, cq=NT, wxq=140,
+                     xoq=256, xo2q=128, q1=CH, qin=224, m1=128, big=2 * HALF, t1=NT, oq=NT))
+SCRATCH.update({"uin": sb(2, F8), "uins": sb(8, "uint8")})
+SEMAPHORES = ["sV", "sT", "sS", "sG", "du", "dx0", "dx1", "dx2", "dv0", "dv1", "dv2", "dv3", "dw", "doff", "dst",
+              "au", "aq", "at", "am", "al", "ao", "ls"]
+
+OP = AluOpType
+AF = ActivationFunctionType
+BIG16 = 201326592.0
+ULP = 1.03125 * 2.0 ** -24
+TINY = 1e-37
+
+
+def sched(g, T):
+    eng = {"V": g.vector, "T": g.tensor, "S": g.scalar, "G": g, "Y": g.sync}
+    cnt = {"V": 0, "T": 0, "S": 0, "G": 0}
+    wr, rd, seen = {}, {}, {}
+
+    def wait(q, reads, writes):
+        req = {}
+        for k in reads:
+            for qq, s, v in wr.get(k, []):
+                req[s] = max(req.get(s, 0), v)
+        for k in writes:
+            for qq, s, v in wr.get(k, []) + rd.get(k, []):
+                if qq != q or q != "T":
+                    req[s] = max(req.get(s, 0), v)
+        for s, v in req.items():
+            if seen.get((q, s), 0) < v:
+                eng[q].wait_ge(T.sem[s], v)
+                seen[(q, s)] = v
+
+    def note(q, s, v, reads, writes):
+        for k in reads:
+            rd.setdefault(k, []).append((q, s, v))
+        for k in writes:
+            wr[k] = [(q, s, v)]
+            rd[k] = []
+
+    def op(q, call, reads, writes):
+        wait(q, reads, writes)
+        cnt[q] += 1
+        call(eng[q]).then_inc(T.sem["s" + q], 1)
+        note(q, "s" + q, cnt[q], reads, writes)
+
+    def dma(q, pairs, s, v, reads, writes):
+        wait(q, reads, writes)
+        for o, i in pairs:
+            eng[q].dma_start(o, i).then_inc(T.sem[s], 16)
+        note("dma", s, v, reads, writes)
+
+    def arrive(s, v, keys):
+        for k in keys:
+            wr[k] = [("far", s, v)]
+    return op, dma, arrive, wait, cnt
+
+
+def rank_program(g, core, T, topo):
+    r = T.rank_of(core)
+    if r is None:
+        return
+    n = len(T.cores)
+    nxt, nx2, prv = T.cores[(r + 1) % n], T.cores[(r + 2) % n], T.cores[(r - 1) % n]
+    op, dma, arrive, wait, cnt = sched(g, T)
+    ps = T.ps
+    loc = [0]
+
+    def half(dst, k):
+        e = topo.engines(core, dst)
+        return e[:len(e) // 2] if k == 0 else e[len(e) // 2:]
+
+    def bits(es):
+        return sum(1 << e for e in es)
+
+    def send(dst, out, src, sem, es, reads):
+        wait("G", reads, [])
+        rid, pid, _ = topo.addr(dst)
+        g.remote_dma(out, src, T.sem[sem], T.sem["ls"], pid, rid, bits(es))
+        loc[0] += len(es)
+
+    def u8(name, a, b):
+        return T[name][:, a:b].bitcast(dt.uint8)
+
+    arrive("au", 8, ["uin", "uins"])
+    arrive("aq", 32, ["qin", "qins"])
+    arrive("at", 16, ["bt", "bts"])
+    arrive("am", 32, ["bm", "bms"])
+    arrive("al", 8, ["lin"])
+    arrive("ao", 8, ["offd"])
+
+    def V(f, reads, writes):
+        op("V", f, reads, writes)
+
+    def S(f, reads, writes):
+        op("S", f, reads, writes)
+
+    def G(f, reads, writes):
+        op("G", f, reads, writes)
+
+    def memset(ap, c, key, after=()):
+        V(lambda e: e.memset(ap, c), list(after), [key])
+
+    def ts(out, in0, s1, o, reads, key):
+        V(lambda e: e.tensor_scalar(out, in0, s1, None, o), reads, [key])
+
+    def tt(out, in0, in1, o, reads, key):
+        V(lambda e: e.tensor_tensor(out, in0, in1, o), reads, [key])
+
+    def cp(out, in_, reads, key):
+        V(lambda e: e.tensor_copy(out, in_), reads, [key])
+
+    def quant(out, a, b, src, reads, key):
+        V(lambda e: e.quantize_mx(T[out][:, a:b], T[out + "s"][:, a:b], src), reads, [key])
+
+    def mm(bank, w, L, l0, R, r0, start, stop, reads):
+        op("T", lambda e: e.matmul_mx(ps[:, 512 * bank:512 * bank + w], T[L][:, l0:l0 + 128], T[L + "s"][:, l0:l0 + 128],
+                                      T[R][:, r0:r0 + w], T[R + "s"][:, r0:r0 + w], start, stop), reads, ["b%d" % bank])
+
+    def B(bank, a, b):
+        return ps[:, 512 * bank + a:512 * bank + b]
+
+    def pick_c(dst, d0, w, src, a, b, off, o0, reads, key):
+        V(lambda e: e.tensor_copy(T[dst][:, d0:d0 + w].bitcast(dt.uint32),
+                                  T[src][:, a:b].bitcast(dt.uint32).indirect(T[off][:, o0:o0 + w // 16])), reads, [key])
+
+    def pick_s(dst, d0, w, src, a, b, off, o0, reads, key):
+        S(lambda e: e.activation(T[dst + "s"][:, d0:d0 + w], T[src + "s"][:, a:b].indirect(T[off][:, o0:o0 + w // 16]),
+                                 AF.Copy), reads, [key])
+
+    def hk(key):
+        return [key + str(i) for i in range(4)]
+
+    dma("Y", [(T.ub[:, 0:8], T.u[:, 0:8])], "du", 16, [], ["ub"])
+    for c in range(3):
+        dma("Y", [(T.xb[:, 512 * c:512 * c + 512], T.x[:, 512 * c:512 * c + 512])], "dx%d" % c, 16, [], ["xb%d" % c])
+
+    imp = {"allow_small_or_imprecise_dtypes": True}
+    memset(T.ub[:, 8:512], 0.0, "ubz")
+    memset(T.ones[:], 1.0, "ones")
+    G(lambda e: e.iota(T.jj[:], [[0, 24], [128, 4]], 0, 1), [], ["jj"])
+    G(lambda e: e.iota(T.kk[:], [[1, 24], [0, 4]], 0, 0), [], ["kk"])
+    G(lambda e: e.affine_select(T.tri[:], T.ones[:], [[1, 128]], OP.is_gt, 0.0, 0, -1), ["ones"], ["tri"])
+    G(lambda e: e.iota(T.pp[:], [[1, 128]], 0, 0, **imp), [], ["pp"])
+    memset(T.z16[:], 0, "z16")
+    memset(T.eb[:], 0.0, "eb")
+    ts(T.j16[:], T.jj[:], 16, OP.add, ["jj"], "j16")
+    ts(T.jk[:], T.jj[:], 4, OP.logical_shift_right, ["jj"], "jk")
+    ts(T.p16[:], T.jj[:, 0:4], 15, OP.bitwise_and, ["jj"], "p16")
+    ts(T.ja[:], T.j16[:], 480, OP.bitwise_and, ["j16"], "ja")
+    ts(T.g3a[:], T.jk[:, 0:16], 11, OP.mult, ["jk"], "g3a")
+    ts(T.p128[:], T.p16[:], 8, OP.mult, ["p16"], "p128")
+    quant("uq", 0, 128, T.ub[:], ["ub", "ubz"], "uq")
+    wait("G", ["uq"], [])
+    rid, pid, _ = topo.addr(prv)
+    e0 = half(prv, 0)
+    g.remote_dma_fused([RemoteDMATransfer(dst_ids=[DstId(rid=rid, pnc=pid)], dma_engine_mask=bits(e0[:4]), remote_sem=T.sem["au"],
+                                          src=u8("uq", 0, 2), dst=u8("uin", 0, 2)),
+                        RemoteDMATransfer(dst_ids=[DstId(rid=rid, pnc=pid)], dma_engine_mask=bits(e0[4:]), remote_sem=T.sem["au"],
+                                          src=T.uqs[:, 0:8], dst=T.uins[:, 0:8])], local_sem=T.sem["ls"])
+    loc[0] += len(e0)
+    G(lambda e: e.affine_select(T.eb[:, 4:516:4], T.ones[:], [[-1, 128]], OP.is_equal, 0.0, 0, 1), ["ones", "eb"], ["ebi"])
+    G(lambda e: e.iota(T.q0[:], [[0, 8], [1, 16]], 0, 0, **imp), [], ["q0"])
+    G(lambda e: e.iota(T.kc[:], [[0, 2], [16, 6], [0, 4]], 0, 0, **imp), [], ["kc"])
+    memset(T.zb[:], 0.0, "zbz")
+    tt(T.jb[:], T.jj[:], T.ja[:], OP.subtract, ["jj", "ja"], "jb")
+    ts(T.g3[:], T.g3a[:], 5, OP.logical_shift_right, ["g3a"], "g3")
+    cp(T.p16f[:], T.p16[:], ["p16"], "p16f")
+    cp(T.ab[:, 0:24], T.ja[:, 0:24], ["ja"], "aba")
+    ts(T.ab2[:, 0:4], T.ja[:, 0:4], float(CH), OP.add, ["ja"], "ab2a")
+    ts(T.g3b[:], T.g3[:], 3, OP.mult, ["g3"], "g3b")
+    tt(T.s4[:], T.p128[:], T.g3[:, 0:4], OP.add, ["p128", "g3"], "s4")
+    cp(T.ab[:, 24:48], T.jb[:, 0:24], ["jb"], "abb")
+    cp(T.ab2[:, 4:8], T.jb[:, 0:4], ["jb"], "ab2b")
+    tt(T.i3[:], T.jk[:, 0:16], T.g3b[:], OP.subtract, ["jk", "g3b"], "i3")
+    for t in range(4):
+        memset(T.zb[:, t:256:16], 1.0, "zb%d" % t, ["zbz"])
+        memset(T.zb[:, 260 + t:768:16], 1.0, "zb%d" % (4 + t), ["zbz"])
+    memset(T.ab[:, 3:48:4], 0.0, "ab", ["aba", "abb"])
+    tt(T.mk1[:], T.i3[:], T.kk[:, 0:16], OP.is_equal, ["i3", "kk"], "mk1a")
+    for c in range(3):
+        quant("t0", 128 * c, 128 * c + 128, T.xb[:, 512 * c:512 * c + 512], ["xb%d" % c], "t0%d" % c)
+    t0 = ["t00", "t01", "t02"]
+    send(nx2, u8("big", T0, T0 + NT), u8("t0", 0, NT), "at", half(nx2, 1), t0)
+    send(nx2, T.bigs[:, T0:T0 + NT], T.t0s[:, 0:NT], "at", half(nx2, 1), [])
+    for z, w, k in (("wx", 560, "wxz"), ("xo", 512, "xoz"), ("zero", 512, "zero"), ("xo2", 512, "xo2z")):
+        G(lambda e, z=z, w=w: e.iota(T[z][:], [[0, w]], 0, 0, **imp), [], [k])
+    memset(T.mk1[:, 3:16:4], 0.0, "mk1", ["mk1a"])
+    quant("zq", 0, 192, T.zb[:], ["zbz"] + ["zb%d" % t for t in range(8)], "zq")
+    ts(T.qm[:], T.q0[:], -7.5, OP.add, ["q0"], "qm")
+    for b in range(4):
+        quant("eq", 128 * b, 128 * b + 128, T.eb[:, 4 - b:516 - b], ["eb", "ebi"], "eq%d" % b)
+    for t in range(4):
+        ts(T.w1b[:, t:512:4], T.pp[:], T.s4[:, t:t + 1], OP.is_equal, ["pp", "s4"], "w1b%d" % t)
+    quant("w1", 0, 128, T.w1b[:], hk("w1b"), "w1")
+    pick_c("ur1", 0, 128, "uin", 0, 2, "z16", 0, ["uin", "uins", "z16"], "ur1")
+    pick_s("ur1", 0, 128, "uin", 0, 2, "z16", 0, ["uin", "uins", "z16"], "ur1s")
+    for c in range(3):
+        memset(T.cmp[:, 512 * c + c:512 * c + 512:4], 0.0, "cz%d" % c)
+    for c in range(3):
+        memset(T.cmp[0:1, 512 * c + c:512 * c + 512:4], -7.5, "cm%d%d" % (c, c), ["cz%d" % c])
+
+    ROW = (0, 6, 7)
+
+    def scores(c, tok, ur, keys, what):
+        if "c" in what:
+            mm(1 + c, 128, tok, 128 * c, ur, 0, True, True, keys)
+        if "r" in what:
+            mm(ROW[c], 128, ur, 0, tok, 128 * c, True, True, keys)
+
+    def order(beside):
+        cp(T.sc[:], ps[:, 512:2048:512], ["b1", "b2", "b3"], "sc")
+        S(lambda e: e.activation(T.dl[:], T.sc[:], AF.Abs, bias=0.0, scale=ULP), ["sc"], ["dl"])
+        S(lambda e: e.activation(T.dl[:], T.dl[:], AF.Copy, bias=TINY), ["dl"], ["dl"])
+        for c in range(3):
+            for t in range(3):
+                if t != c:
+                    ts(T.cmp[:, 512 * c + t:512 * c + 512:4], B(ROW[c], 0, 128), T.sc[:, t:t + 1], OP.is_le if t < c else OP.is_lt,
+                       ["b%d" % ROW[c], "sc"], "cm%d%d" % (c, t))
+        for c in range(3):
+            S(lambda e, c=c: e.activation(T.mt[:, 128 * c:128 * c + 128], T.tri[:], AF.Identity, bias=T.sc[:, c:c + 1],
+                                          scale=T.dl[:, c:c + 1]), ["tri", "sc", "dl"], ["mt%d" % c])
+            tt(T.cmp[:, 512 * c + 3:512 * c + 512:4], B(ROW[c], 0, 128), T.mt[:, 128 * c:128 * c + 128], OP.is_lt,
+               ["b%d" % ROW[c], "mt%d" % c], "cm%d3" % c)
+            quant("cq", 128 * c, 128 * c + 128, T.cmp[:, 512 * c:512 * c + 512], ["cm%d%d" % (c, t) for t in range(4)], "cq%d" % c)
+            beside(c)
+        for c in range(3):
+            mm(4, 128, "cq", 128 * c, "zq", (0, 64, 2)[c], c == 0, c == 2, ["cq%d" % c, "zq"])
+            if c == 0:
+                beside(3)
+
+    def onehot():
+        V(lambda e: e.tensor_scalar(T.kl[:, 0:48], B(4, 0, 48), BIG16, BIG16, OP.add, OP.subtract), ["b4"], ["kl"])
+        tt(T.x0[:], T.kl[:, 0:48], T.kc[:], OP.is_equal, ["kl", "kc"], "x0")
+        for t in range(3):
+            V(lambda e, t=t: e.tensor_scalar(T.wx[:, 48 + t:560:4], T.qm[:], T.kl[:, t:t + 1], B(4, t, t + 1), OP.add, OP.is_equal),
+              ["kl", "qm", "b4", "wxz"], ["wx%d" % t])
+        tt(T.wx[:, 0:48], T.x0[:], T.ab[:], OP.mult, ["x0", "ab", "wxz"], "wxx")
+        quant("wxq", 0, 140, T.wx[:], ["wxz", "wx0", "wx1", "wx2", "wxx"], "wxq")
+
+    def list_mm(bank):
+        mm(bank, 128, "wxq", 12, "wxq", 0, True, False, ["wxq"])
+        mm(bank, 128, "wxq", 12, "wxq", 6, False, True, ["wxq"])
+
+    def R(i, bank, q, q0, w, out, w2, keys):
+        mm(bank, w, "vq", 128 * i, q, q0, True, True, keys + ["vq%d" % i])
+        S(lambda e: e.activation(T[out][:, w2 * i:w2 * i + w2], B(bank, 0, w2), AF.Relu, scale=0.05), ["b%d" % bank], [out + str(i)])
+
+    def D(i, bank, q, q0, w, keys):
+        mm(bank, w, "eq", 128 * i, q, q0, True, True, keys + ["eq%d" % i])
+
+    def add(i, bank, h, c0, w, hr, key):
+        tt(T[h][:, 4 * c0 + i:4 * (c0 + w):4], T[hr][:, w * i:w * i + w], B(bank, 0, w), OP.add, [hr + str(i), "b%d" % bank], key + str(i))
+
+    def ycopy(bank, a, w, reads):
+        mm(bank, max(w, 128), "wq", 0, "big", a, True, True, ["wq"] + reads)
+        S(lambda e: e.activation(T.yw[:, a:a + w], B(bank, 0, w), AF.Copy), ["b%d" % bank], ["yw%d" % a])
+
+    for w in "cr":
+        for c in range(3):
+            scores(c, "t0", "ur1", ["t0%d" % c, "ur1", "ur1s"], w)
+    order(lambda c: None)
+    for i in range(4):
+        dma("Y", [(T.vb[:, 512 * i:512 * i + 512], T.v[:, 512 * i:512 * i + 512])], "dv%d" % i, 16, ["sc"], ["vb%d" % i])
+    onehot()
+    list_mm(5)
+    ts(T.rkp[:], B(4, 0, 4), 7.5, OP.add, ["b4"], "rkp")
+    ts(T.sel[:], B(4, 0, 8), CH - 7.5, OP.is_lt, ["b4"], "sel")
+    tt(T.kl[:, 48:52], T.rkp[:], T.kl[:, 44:48], OP.subtract, ["rkp", "kl"], "kl2")
+    cp(T.lst1[:], B(5, 0, 6), ["b5"], "lst1")
+    pick_c("q1", 0, CH, "t0", 0, NT, "lst1", 0, t0 + ["lst1"], "q1")
+    pick_s("q1", 0, CH, "t0", 0, NT, "lst1", 0, t0 + ["lst1"], "q1s")
+    send(nxt, u8("qin", 0, CH), u8("q1", 0, CH), "aq", topo.engines(core, nxt), ["q1"])
+    send(nxt, T.qins[:, 0:CH], T.q1s[:, 0:CH], "aq", topo.engines(core, nxt), ["q1s"])
+    tt(T.hl[:], T.kl[:, 44:52], T.ab2[:], OP.subtract, ["kl", "kl2", "ab2a", "ab2b"], "hl")
+    tt(T.hm[:], T.hl[:], T.sel[:], OP.mult, ["hl", "sel"], "hm")
+    tt(T.hn[:], T.hm[:], T.ab2[:], OP.add, ["hm", "ab2a", "ab2b"], "hn")
+    for k in range(2):
+        for t in range(3):
+            ts(T.xo[:, 16 * k + t:16 * k + 16:4], T.mk1[:, t:16:4], T.hn[:, 4 * k + t:4 * k + t + 1], OP.mult,
+               ["hn", "mk1", "xoz"], "xo%d%d" % (k, t))
+    quant("xoq", 0, 128, T.xo[:], ["xoz"] + ["xo%d%d" % (k, t) for k in range(2) for t in range(3)], "xoq")
+    quant("xoq", 128, 256, T.zero[:], ["zero"], "xoqz")
+
+    def D0(b):
+        D(b, b, "big", T0, NT, ["bt", "bts"])
+    D0(0), D0(1)
+    mm(6, 128, "w1", 0, "xoq", 0, True, False, ["xoq", "xoqz", "w1"])
+    mm(6, 128, "w1", 0, "xoq", 4, False, True, ["xoq", "xoqz", "w1"])
+    D0(2), D0(3)
+    quant("qin", 96, 224, T.zero[:], ["zero"], "qinz")
+    cp(T.offc[:], B(6, 0, 3), ["b6"], "offc")
+    send(nx2, T.offd[:], T.offc[:], "ao", half(nx2, 0), ["offc"])
+    send(nx2, T.lin[:], T.lst1[:], "al", half(nx2, 0), ["lst1"])
+    for i in range(4):
+        quant("vq", 128 * i, 128 * i + 128, T.vb[:, 512 * i:512 * i + 512], ["vb%d" % i], "vq%d" % i)
+    memset(T.hb[:, 4 * CH:512], 0.0, "hbz")
+
+    qk = ["qin", "qins", "qinz"]
+
+    def RB(i, bank):
+        R(i, bank, "qin", 0, 128, "hrb", CH, qk)
+
+    def DB(i, bank):
+        D(i, bank, "qin", 0, 128, qk)
+
+    def AB(i, bank):
+        add(i, bank, "hb", 0, CH, "hrb", "hb")
+    RB(0, 4), RB(1, 5), DB(0, 6), RB(2, 4), DB(1, 7), RB(3, 5)
+    AB(0, 6), DB(2, 6), AB(1, 7), DB(3, 7), AB(2, 6), AB(3, 7)
+    quant("m1", 0, 128, T.hb[:], ["hbz"] + hk("hb"), "m1")
+    send(nxt, u8("big", HALF, HALF + CH), u8("m1", 0, CH), "am", topo.engines(core, nxt), ["m1"])
+    send(nxt, T.bigs[:, HALF:HALF + CH], T.m1s[:, 0:CH], "am", topo.engines(core, nxt), [])
+    dma("Y", [(T.wb[:], T.w[:])], "dw", 16, ["qin"], ["wb"])
+    dma("Y", [(T.off1[16 * h:16 * h + 16, :], T.offd[:]) for h in range(8)], "doff", 128, ["offd"], ["off1"])
+    for i in range(4):
+        R(i, 4 + i, "big", T0, NT, "hr0", NT, ["bt", "bts"])
+    for i in range(4):
+        ts(T.w2b[:, i:512:4], T.q0[:], T.p16f[:, i:i + 1], OP.is_equal, ["q0", "p16f"], "w2b%d" % i)
+    tt(T.mk2[:], T.jk[:], T.kk[:], OP.is_equal, ["jk", "kk"], "mk2")
+    quant("w2", 0, 128, T.w2b[:], hk("w2b"), "w2")
+    V(lambda e: e.tensor_scalar(T.thr[:], T.mk2[:], -400.0, CH - 7.5 + 400.0, OP.mult, OP.add), ["mk2"], ["thr"])
+    for i in range(4):
+        add(i, i, "hx", CH, NT, "hr0", "h0")
+        if i == 0:
+            pick_c("ur2", 0, 128, "uq", 0, 2, "z16", 0, ["uq", "z16"], "ur2")
+            pick_s("ur2", 0, 128, "uq", 0, 2, "z16", 0, ["uq", "z16"], "ur2s")
+            quant("wq", 0, 128, T.wb[:], ["wb"], "wq")
+            ycopy(4, T0, NT, ["bt", "bts"])
+    quant("big", CH, HALF, T.hx[:, 4 * CH:4 * HALF], hk("h0"), "bh0")
+    cp(T.lif[:, 0:6], T.lin[:], ["lin"], "lif1")
+    cp(T.off1f[:], T.off1[:], ["off1"], "off1f")
+    stores = [0]
+
+    def store(q, pairs, reads):
+        dma(q, pairs, "dst", 0, reads, [])
+        stores[0] += 16 * len(pairs)
+    store("Y", [(T.li[0:1, 16 * k:16 * k + 16], T.lif[0:16, k:k + 1]) for k in range(6)], ["lif1"])
+
+    mk = ["bt", "bts", "bm", "bms"]
+    for c in range(3):
+        pick_c("t1", 128 * c, 128, "big", HALF, 2 * HALF, "off1", 8 * c, mk + ["off1"], "t1c%d" % c)
+        pick_s("t1", 128 * c, 128, "big", HALF, 2 * HALF, "off1", 8 * c, mk + ["off1"], "t1s%d" % c)
+        scores(c, "t1", "ur2", ["t1c%d" % c, "t1s%d" % c, "ur2", "ur2s"], "cr")
+
+    def N(what, i, bank):
+        if what == "D":
+            D(i, bank, "big", HALF, 128, mk)
+        else:
+            R(i, bank, "big", HALF, 128, "hr1", CH, mk)
+
+    def beside(c):
+        if c == 0:
+            N("D", 0, 2), N("R", 0, 1), N("D", 1, 3)
+        elif c == 1:
+            N("R", 1, 5), N("R", 2, 1)
+        elif c == 2:
+            N("R", 3, 5), N("D", 2, 0)
+        else:
+            N("D", 3, 6)
+    order(beside)
+    add(0, 2, "hx", 0, CH, "hr1", "h1")
+    add(1, 3, "hx", 0, CH, "hr1", "h1")
+    for t in range(3):
+        V(lambda e, t=t: e.tensor_scalar(T.xo2[:, t:96:4], T.thr[:, t:96:4], B(4, t, t + 1), float(HALF), OP.is_le, OP.mult),
+          ["thr", "b4", "xo2z"], ["xo2%d" % t])
+    quant("xo2q", 0, 128, T.xo2[:], ["xo2z", "xo20", "xo21", "xo22"], "xo2q")
+    ycopy(2, 128, HALF - 128, ["bh0"])
+    mm(1, 128, "w2", 0, "xo2q", 0, True, True, ["xo2q", "w2"])
+    ycopy(3, HALF, CH, mk)
+    add(2, 0, "hx", 0, CH, "hr1", "h1")
+    add(3, 6, "hx", 0, CH, "hr1", "h1")
+    quant("big", 0, 128, T.hx[:, 0:512], hk("h0") + hk("h1") + ["bh0"], "bh1")
+    ycopy(5, 0, 128, ["bh1"])
+    tt(T.off2f[:], T.off1f[:], B(1, 0, 24), OP.add, ["off1f", "b1"], "off2f")
+    cp(T.off2[:], T.off2f[:], ["off2f"], "off2")
+    al = ["bh0", "bh1", "off2"] + mk
+    yk = ["yw%d" % a for a in (0, 128, HALF, T0)]
+
+    def pick_y(q, a, b, key):
+        src = T.yw[:].indirect(T.off2[:, a // 16:b // 16])
+        if q == "V":
+            cp(T.yb[:, a:b], src, yk + ["off2"], key)
+        else:
+            S(lambda e: e.activation(T.yb[:, a:b], src, AF.Copy), yk + ["off2"], [key])
+    for c in range(3):
+        pick_c("oq", 128 * c, 128, "big", 0, 2 * HALF, "off2", 8 * c, al, "oq%d" % c)
+        store("Y", [(T.oc[:, 512 * c:512 * c + 512], u8("oq", 128 * c, 128 * c + 128))], ["oq%d" % c])
+    pick_y("S", 0, 192, "yb0")
+    store("Y", [(T.y[:, 0:192], T.yb[:, 0:192])], ["yb0"])
+    pick_s("oq", 0, NT, "big", 0, 2 * HALF, "off2", 0, al, "oqs")
+    store("S", [(T.osc[4 * k:4 * k + 4, :], T.oqs[32 * k:32 * k + 4, :]) for k in range(4)], ["oqs"])
+    pick_y("V", 192, 384, "yb1")
+    store("Y", [(T.y[:, 192:384], T.yb[:, 192:384])], ["yb1"])
+    onehot()
+    list_mm(7)
+    cp(T.lif[:, 6:12], B(7, 0, 6), ["b7"], "lif2")
+    store("Y", [(T.li[1:2, 16 * k:16 * k + 16], T.lif[0:16, 6 + k:7 + k]) for k in range(6)], ["lif2"])
+
+    for q in ("V", "T", "S", "G"):
+        g.wait_ge(T.sem["s" + q], cnt[q])
+    g.wait_ge(T.sem["ls"], loc[0])
+    g.wait_ge(T.sem["dst"], stores[0])

@@ -23,7 +23,7 @@ def codes(**names):
 SCRATCH = {
     "ps": ("psum", [128, 4096], "float32"),
     "ub": sb(512, "bfloat16"), "xb": sb(4 * NT, "bfloat16"), "vb": sb(2048, "bfloat16"), "wb": sb(512, "bfloat16"),
-    "ones": sb(128, "bfloat16"), "zero": sb(512, "bfloat16"), "z16": sb(8, "uint16"), "eb": sb(520, "bfloat16"),
+    "ones": sb(128, "bfloat16"), "z16": sb(8, "uint16"), "eb": sb(520, "bfloat16"), "zi": sb(256, "bfloat16"),
     "tri": sb(128, "bfloat16"), "q0": sb(128, "bfloat16"), "qm": sb(128, "bfloat16"), "pp": sb(128, "bfloat16"),
     "kc": sb(48, "float32"), "jj": sb(96, "int32"), "kk": sb(96, "int32"), "j16": sb(96, "int32"),
     "ja": sb(96, "int32"), "jb": sb(96, "int32"), "jk": sb(96, "int32"), "g3": sb(16, "int32"), "g3a": sb(16, "int32"),
@@ -34,15 +34,15 @@ SCRATCH = {
     "sc": sb(3, "float32"), "dl": sb(3, "float32"), "mt": sb(NT, "float32"), "cmp": sb(4 * NT, "bfloat16"),
     "kl": sb(52, "float32"), "x0": sb(48, "float32"), "wx": sb(560, "bfloat16"),
     "sel": sb(8, "float32"), "rkp": sb(4, "float32"), "hl": sb(8, "float32"), "hm": sb(8, "float32"), "hn": sb(8, "float32"),
-    "xo": sb(512, "bfloat16"), "xo2": sb(512, "bfloat16"),
+    "xo": sb(544, "bfloat16"),
     "lst1": sb(6, "uint16"), "offc": sb(3, "uint16"), "off2f": sb(24, "float32"), "off2": sb(24, "uint16"),
     "lin": sb(6, "uint16"), "offd": ("dram", [128, 3], "uint16"), "off1": sb(24, "uint16"), "off1f": sb(24, "float32"),
     "hrb": sb(4 * CH, "float32"), "hr0": sb(4 * NT, "float32"), "hr1": sb(4 * CH, "float32"),
     "hb": sb(512, "bfloat16"), "hx": sb(4 * HALF, "bfloat16"),
     "yb": sb(NT, "float32"), "yw": sb(2 * HALF, "float32"), "lif": sb(12, "float32"),
 }
-SCRATCH.update(codes(uq=128, ur1=128, ur2=128, t0=NT, vq=512, wq=128, eq=512, w1=128, w2=128, zq=192, cq=NT, wxq=140,
-                     xoq=256, xo2q=128, q1=CH, qin=224, m1=128, big=2 * HALF, t1=NT, oq=NT))
+SCRATCH.update(codes(uq=128, ur1=128, ur2=128, t0=NT, vq=512, wq=128, qe=CH + 512, w1=128, w2=128, zq=192, cq=NT, wxq=140,
+                     xoq=136, q1=CH, m1=128, big=2 * HALF, t1=NT, oq=NT))
 SCRATCH.update({"uin": sb(2, F8), "uins": sb(8, "uint8")})
 SEMAPHORES = ["sV", "sT", "sS", "sG", "du", "dx0", "dx1", "dx2", "dv0", "dv1", "dv2", "dv3", "dw", "doff", "dst",
               "au", "aq", "at", "am", "al", "ao", "ls"]
@@ -125,9 +125,9 @@ def rank_program(g, core, T, topo):
         return T[name][:, a:b].bitcast(dt.uint8)
 
     arrive("au", 8, ["uin", "uins"])
-    arrive("aq", 32, ["qin", "qins"])
-    arrive("at", 16, ["bt", "bts"])
-    arrive("am", 32, ["bm", "bms"])
+    arrive("aq", 32, ["qin"])
+    arrive("at", 16, ["bt"])
+    arrive("am", 32, ["bm"])
     arrive("al", 8, ["lin"])
     arrive("ao", 8, ["offd"])
 
@@ -142,6 +142,9 @@ def rank_program(g, core, T, topo):
 
     def memset(ap, c, key, after=()):
         V(lambda e: e.memset(ap, c), list(after), [key])
+
+    def iota(ap, pattern, key, cm=0):
+        G(lambda e: e.iota(ap, pattern, 0, cm, allow_small_or_imprecise_dtypes=True), [], [key])
 
     def ts(out, in0, s1, o, reads, key):
         V(lambda e: e.tensor_scalar(out, in0, s1, None, o), reads, [key])
@@ -170,20 +173,19 @@ def rank_program(g, core, T, topo):
         S(lambda e: e.activation(T[dst + "s"][:, d0:d0 + w], T[src + "s"][:, a:b].indirect(T[off][:, o0:o0 + w // 16]),
                                  AF.Copy), reads, [key])
 
-    def hk(key):
-        return [key + str(i) for i in range(4)]
+    def hk(key, k=4):
+        return [key + str(i) for i in range(k)]
 
     dma("Y", [(T.ub[:, 0:8], T.u[:, 0:8])], "du", 16, [], ["ub"])
     for c in range(3):
         dma("Y", [(T.xb[:, 512 * c:512 * c + 512], T.x[:, 512 * c:512 * c + 512])], "dx%d" % c, 16, [], ["xb%d" % c])
 
-    imp = {"allow_small_or_imprecise_dtypes": True}
     memset(T.ub[:, 8:512], 0.0, "ubz")
     memset(T.ones[:], 1.0, "ones")
     G(lambda e: e.iota(T.jj[:], [[0, 24], [128, 4]], 0, 1), [], ["jj"])
     G(lambda e: e.iota(T.kk[:], [[1, 24], [0, 4]], 0, 0), [], ["kk"])
+    iota(T.zi[:], [[0, 16], [1, 4], [0, 4]], "zi")
     G(lambda e: e.affine_select(T.tri[:], T.ones[:], [[1, 128]], OP.is_gt, 0.0, 0, -1), ["ones"], ["tri"])
-    G(lambda e: e.iota(T.pp[:], [[1, 128]], 0, 0, **imp), [], ["pp"])
     memset(T.z16[:], 0, "z16")
     memset(T.eb[:], 0.0, "eb")
     ts(T.j16[:], T.jj[:], 16, OP.add, ["jj"], "j16")
@@ -202,9 +204,7 @@ def rank_program(g, core, T, topo):
                                           src=T.uqs[:, 0:8], dst=T.uins[:, 0:8])], local_sem=T.sem["ls"])
     loc[0] += len(e0)
     G(lambda e: e.affine_select(T.eb[:, 4:516:4], T.ones[:], [[-1, 128]], OP.is_equal, 0.0, 0, 1), ["ones", "eb"], ["ebi"])
-    G(lambda e: e.iota(T.q0[:], [[0, 8], [1, 16]], 0, 0, **imp), [], ["q0"])
-    G(lambda e: e.iota(T.kc[:], [[0, 2], [16, 6], [0, 4]], 0, 0, **imp), [], ["kc"])
-    memset(T.zb[:], 0.0, "zbz")
+    iota(T.pp[:], [[1, 128]], "pp")
     tt(T.jb[:], T.jj[:], T.ja[:], OP.subtract, ["jj", "ja"], "jb")
     ts(T.g3[:], T.g3a[:], 5, OP.logical_shift_right, ["g3a"], "g3")
     cp(T.p16f[:], T.p16[:], ["p16"], "p16f")
@@ -215,56 +215,53 @@ def rank_program(g, core, T, topo):
     cp(T.ab[:, 24:48], T.jb[:, 0:24], ["jb"], "abb")
     cp(T.ab2[:, 4:8], T.jb[:, 0:4], ["jb"], "ab2b")
     tt(T.i3[:], T.jk[:, 0:16], T.g3b[:], OP.subtract, ["jk", "g3b"], "i3")
-    for t in range(4):
-        memset(T.zb[:, t:256:16], 1.0, "zb%d" % t, ["zbz"])
-        memset(T.zb[:, 260 + t:768:16], 1.0, "zb%d" % (4 + t), ["zbz"])
+    for k in range(2):
+        ts(T.zb[:, 256 * k:256 * k + 256], T.zi[:], float(k), OP.is_equal, ["zi"], "zb%d" % k)
+    memset(T.zb[:, 512:768], 0.0, "zb2")
     memset(T.ab[:, 3:48:4], 0.0, "ab", ["aba", "abb"])
     tt(T.mk1[:], T.i3[:], T.kk[:, 0:16], OP.is_equal, ["i3", "kk"], "mk1a")
+    memset(T.wx[:], 0.0, "wxz")
+    memset(T.mk1[:, 3:16:4], 0.0, "mk1", ["mk1a"])
     for c in range(3):
         quant("t0", 128 * c, 128 * c + 128, T.xb[:, 512 * c:512 * c + 512], ["xb%d" % c], "t0%d" % c)
-    t0 = ["t00", "t01", "t02"]
+    t0 = hk("t0", 3)
     send(nx2, u8("big", T0, T0 + NT), u8("t0", 0, NT), "at", half(nx2, 1), t0)
     send(nx2, T.bigs[:, T0:T0 + NT], T.t0s[:, 0:NT], "at", half(nx2, 1), [])
-    for z, w, k in (("wx", 560, "wxz"), ("xo", 512, "xoz"), ("zero", 512, "zero"), ("xo2", 512, "xo2z")):
-        G(lambda e, z=z, w=w: e.iota(T[z][:], [[0, w]], 0, 0, **imp), [], [k])
-    memset(T.mk1[:, 3:16:4], 0.0, "mk1", ["mk1a"])
-    quant("zq", 0, 192, T.zb[:], ["zbz"] + ["zb%d" % t for t in range(8)], "zq")
-    ts(T.qm[:], T.q0[:], -7.5, OP.add, ["q0"], "qm")
+    for c in range(3):
+        G(lambda e, c=c: e.affine_select(T.cmp[:, 512 * c + c:512 * c + 512:4], T.wx[:, 0:128], [[0, 128]], OP.not_equal, -7.5, 0, 1),
+          ["wxz"], ["cm%d%d" % (c, c)])
+    iota(T.kc[:], [[0, 2], [16, 6], [0, 4]], "kc")
+    iota(T.q0[:], [[0, 8], [1, 16]], "q0")
+    iota(T.xo[:], [[0, 544]], "xoz")
+    quant("zq", 0, 192, T.zb[:], hk("zb", 3), "zq")
     for b in range(4):
-        quant("eq", 128 * b, 128 * b + 128, T.eb[:, 4 - b:516 - b], ["eb", "ebi"], "eq%d" % b)
-    for t in range(4):
-        ts(T.w1b[:, t:512:4], T.pp[:], T.s4[:, t:t + 1], OP.is_equal, ["pp", "s4"], "w1b%d" % t)
-    quant("w1", 0, 128, T.w1b[:], hk("w1b"), "w1")
+        quant("qe", CH + 128 * b, CH + 128 * b + 128, T.eb[:, 4 - b:516 - b], ["eb", "ebi"], "eq%d" % b)
     pick_c("ur1", 0, 128, "uin", 0, 2, "z16", 0, ["uin", "uins", "z16"], "ur1")
     pick_s("ur1", 0, 128, "uin", 0, 2, "z16", 0, ["uin", "uins", "z16"], "ur1s")
-    for c in range(3):
-        memset(T.cmp[:, 512 * c + c:512 * c + 512:4], 0.0, "cz%d" % c)
-    for c in range(3):
-        memset(T.cmp[0:1, 512 * c + c:512 * c + 512:4], -7.5, "cm%d%d" % (c, c), ["cz%d" % c])
+    for t in range(4):
+        ts(T.w1b[:, t:512:4], T.pp[:], T.s4[:, t:t + 1], OP.is_equal, ["pp", "s4"], "w1b%d" % t)
 
     ROW = (0, 6, 7)
 
-    def scores(c, tok, ur, keys, what):
-        if "c" in what:
-            mm(1 + c, 128, tok, 128 * c, ur, 0, True, True, keys)
-        if "r" in what:
-            mm(ROW[c], 128, ur, 0, tok, 128 * c, True, True, keys)
+    def scores(c, tok, ur, keys):
+        mm(1 + c, 128, tok, 128 * c, ur, 0, True, True, keys)
+        mm(ROW[c], 128, ur, 0, tok, 128 * c, True, True, keys)
 
     def order(beside):
+        def against(c, t, col, key):
+            ts(T.cmp[:, 512 * c + t:512 * c + 512:4], B(ROW[c], 0, 128), col, OP.is_le if t < c else OP.is_lt,
+               ["b%d" % ROW[c], key], "cm%d%d" % (c, t))
+        against(0, 1, B(2, 0, 1), "b2"), against(1, 0, B(1, 0, 1), "b1")
         cp(T.sc[:], ps[:, 512:2048:512], ["b1", "b2", "b3"], "sc")
-        S(lambda e: e.activation(T.dl[:], T.sc[:], AF.Abs, bias=0.0, scale=ULP), ["sc"], ["dl"])
-        S(lambda e: e.activation(T.dl[:], T.dl[:], AF.Copy, bias=TINY), ["dl"], ["dl"])
-        for c in range(3):
-            for t in range(3):
-                if t != c:
-                    ts(T.cmp[:, 512 * c + t:512 * c + 512:4], B(ROW[c], 0, 128), T.sc[:, t:t + 1], OP.is_le if t < c else OP.is_lt,
-                       ["b%d" % ROW[c], "sc"], "cm%d%d" % (c, t))
+        S(lambda e: e.activation(T.dl[:], T.sc[:], AF.Abs, bias=TINY, scale=ULP), ["sc"], ["dl"])
+        for c, t in ((0, 2), (1, 2), (2, 0), (2, 1)):
+            against(c, t, T.sc[:, t:t + 1], "sc")
         for c in range(3):
             S(lambda e, c=c: e.activation(T.mt[:, 128 * c:128 * c + 128], T.tri[:], AF.Identity, bias=T.sc[:, c:c + 1],
                                           scale=T.dl[:, c:c + 1]), ["tri", "sc", "dl"], ["mt%d" % c])
             tt(T.cmp[:, 512 * c + 3:512 * c + 512:4], B(ROW[c], 0, 128), T.mt[:, 128 * c:128 * c + 128], OP.is_lt,
                ["b%d" % ROW[c], "mt%d" % c], "cm%d3" % c)
-            quant("cq", 128 * c, 128 * c + 128, T.cmp[:, 512 * c:512 * c + 512], ["cm%d%d" % (c, t) for t in range(4)], "cq%d" % c)
+            quant("cq", 128 * c, 128 * c + 128, T.cmp[:, 512 * c:512 * c + 512], hk("cm%d" % c), "cq%d" % c)
             beside(c)
         for c in range(3):
             mm(4, 128, "cq", 128 * c, "zq", (0, 64, 2)[c], c == 0, c == 2, ["cq%d" % c, "zq"])
@@ -277,7 +274,7 @@ def rank_program(g, core, T, topo):
         for t in range(3):
             V(lambda e, t=t: e.tensor_scalar(T.wx[:, 48 + t:560:4], T.qm[:], T.kl[:, t:t + 1], B(4, t, t + 1), OP.add, OP.is_equal),
               ["kl", "qm", "b4", "wxz"], ["wx%d" % t])
-        tt(T.wx[:, 0:48], T.x0[:], T.ab[:], OP.mult, ["x0", "ab", "wxz"], "wxx")
+        tt(T.wx[:, 0:48], T.x0[:], T.ab[:], OP.mult, ["x0", "ab", "wxz", "cm00", "cm11", "cm22"], "wxx")
         quant("wxq", 0, 140, T.wx[:], ["wxz", "wx0", "wx1", "wx2", "wxx"], "wxq")
 
     def list_mm(bank):
@@ -289,7 +286,7 @@ def rank_program(g, core, T, topo):
         S(lambda e: e.activation(T[out][:, w2 * i:w2 * i + w2], B(bank, 0, w2), AF.Relu, scale=0.05), ["b%d" % bank], [out + str(i)])
 
     def D(i, bank, q, q0, w, keys):
-        mm(bank, w, "eq", 128 * i, q, q0, True, True, keys + ["eq%d" % i])
+        mm(bank, w, "qe", CH + 128 * i, q, q0, True, True, keys + ["eq%d" % i])
 
     def add(i, bank, h, c0, w, hr, key):
         tt(T[h][:, 4 * c0 + i:4 * (c0 + w):4], T[hr][:, w * i:w * i + w], B(bank, 0, w), OP.add, [hr + str(i), "b%d" % bank], key + str(i))
@@ -298,53 +295,54 @@ def rank_program(g, core, T, topo):
         mm(bank, max(w, 128), "wq", 0, "big", a, True, True, ["wq"] + reads)
         S(lambda e: e.activation(T.yw[:, a:a + w], B(bank, 0, w), AF.Copy), ["b%d" % bank], ["yw%d" % a])
 
-    for w in "cr":
-        for c in range(3):
-            scores(c, "t0", "ur1", ["t0%d" % c, "ur1", "ur1s"], w)
+    for c in range(3):
+        scores(c, "t0", "ur1", ["t0%d" % c, "ur1", "ur1s"])
     order(lambda c: None)
     for i in range(4):
         dma("Y", [(T.vb[:, 512 * i:512 * i + 512], T.v[:, 512 * i:512 * i + 512])], "dv%d" % i, 16, ["sc"], ["vb%d" % i])
+    ts(T.qm[:], T.q0[:], -7.5, OP.add, ["q0"], "qm")
+    memset(T.hb[:, 4 * CH:512], 0.0, "hbz")
     onehot()
     list_mm(5)
     ts(T.rkp[:], B(4, 0, 4), 7.5, OP.add, ["b4"], "rkp")
     ts(T.sel[:], B(4, 0, 8), CH - 7.5, OP.is_lt, ["b4"], "sel")
     tt(T.kl[:, 48:52], T.rkp[:], T.kl[:, 44:48], OP.subtract, ["rkp", "kl"], "kl2")
+    tt(T.hl[:], T.kl[:, 44:52], T.ab2[:], OP.subtract, ["kl", "kl2", "ab2a", "ab2b"], "hl")
     cp(T.lst1[:], B(5, 0, 6), ["b5"], "lst1")
     pick_c("q1", 0, CH, "t0", 0, NT, "lst1", 0, t0 + ["lst1"], "q1")
     pick_s("q1", 0, CH, "t0", 0, NT, "lst1", 0, t0 + ["lst1"], "q1s")
-    send(nxt, u8("qin", 0, CH), u8("q1", 0, CH), "aq", topo.engines(core, nxt), ["q1"])
-    send(nxt, T.qins[:, 0:CH], T.q1s[:, 0:CH], "aq", topo.engines(core, nxt), ["q1s"])
-    tt(T.hl[:], T.kl[:, 44:52], T.ab2[:], OP.subtract, ["kl", "kl2", "ab2a", "ab2b"], "hl")
+    send(nxt, u8("qe", 0, CH), u8("q1", 0, CH), "aq", topo.engines(core, nxt), ["q1"])
+    send(nxt, T.qes[:, 0:CH], T.q1s[:, 0:CH], "aq", topo.engines(core, nxt), ["q1s"])
     tt(T.hm[:], T.hl[:], T.sel[:], OP.mult, ["hl", "sel"], "hm")
+    quant("w1", 0, 128, T.w1b[:], hk("w1b"), "w1")
     tt(T.hn[:], T.hm[:], T.ab2[:], OP.add, ["hm", "ab2a", "ab2b"], "hn")
     for k in range(2):
         for t in range(3):
             ts(T.xo[:, 16 * k + t:16 * k + 16:4], T.mk1[:, t:16:4], T.hn[:, 4 * k + t:4 * k + t + 1], OP.mult,
                ["hn", "mk1", "xoz"], "xo%d%d" % (k, t))
-    quant("xoq", 0, 128, T.xo[:], ["xoz"] + ["xo%d%d" % (k, t) for k in range(2) for t in range(3)], "xoq")
-    quant("xoq", 128, 256, T.zero[:], ["zero"], "xoqz")
+    quant("xoq", 0, 136, T.xo[:], ["xoz"] + hk("xo0", 3) + hk("xo1", 3), "xoq")
 
     def D0(b):
-        D(b, b, "big", T0, NT, ["bt", "bts"])
+        D(b, b, "big", T0, NT, ["bt"])
     D0(0), D0(1)
-    mm(6, 128, "w1", 0, "xoq", 0, True, False, ["xoq", "xoqz", "w1"])
-    mm(6, 128, "w1", 0, "xoq", 4, False, True, ["xoq", "xoqz", "w1"])
+    mm(6, 128, "w1", 0, "xoq", 0, True, False, ["xoq", "w1"])
+    mm(6, 128, "w1", 0, "xoq", 4, False, True, ["xoq", "w1"])
     D0(2), D0(3)
-    quant("qin", 96, 224, T.zero[:], ["zero"], "qinz")
+    tt(T.mk2[:], T.jk[:], T.kk[:], OP.is_equal, ["jk", "kk"], "mk2")
+    for t in range(4):
+        ts(T.w2b[:, t:512:4], T.q0[:], T.p16f[:, t:t + 1], OP.is_equal, ["q0", "p16f"], "w2b%d" % t)
     cp(T.offc[:], B(6, 0, 3), ["b6"], "offc")
     send(nx2, T.offd[:], T.offc[:], "ao", half(nx2, 0), ["offc"])
     send(nx2, T.lin[:], T.lst1[:], "al", half(nx2, 0), ["lst1"])
     for i in range(4):
         quant("vq", 128 * i, 128 * i + 128, T.vb[:, 512 * i:512 * i + 512], ["vb%d" % i], "vq%d" % i)
-    memset(T.hb[:, 4 * CH:512], 0.0, "hbz")
-
-    qk = ["qin", "qins", "qinz"]
+    V(lambda e: e.tensor_scalar(T.thr[:], T.mk2[:], -400.0, CH - 7.5 + 400.0, OP.mult, OP.add), ["mk2"], ["thr"])
 
     def RB(i, bank):
-        R(i, bank, "qin", 0, 128, "hrb", CH, qk)
+        R(i, bank, "qe", 0, 128, "hrb", CH, ["qin", "eq0"])
 
     def DB(i, bank):
-        D(i, bank, "qin", 0, 128, qk)
+        D(i, bank, "qe", 0, 128, ["qin", "eq0"])
 
     def AB(i, bank):
         add(i, bank, "hb", 0, CH, "hrb", "hb")
@@ -356,22 +354,17 @@ def rank_program(g, core, T, topo):
     dma("Y", [(T.wb[:], T.w[:])], "dw", 16, ["qin"], ["wb"])
     dma("Y", [(T.off1[16 * h:16 * h + 16, :], T.offd[:]) for h in range(8)], "doff", 128, ["offd"], ["off1"])
     for i in range(4):
-        R(i, 4 + i, "big", T0, NT, "hr0", NT, ["bt", "bts"])
-    for i in range(4):
-        ts(T.w2b[:, i:512:4], T.q0[:], T.p16f[:, i:i + 1], OP.is_equal, ["q0", "p16f"], "w2b%d" % i)
-    tt(T.mk2[:], T.jk[:], T.kk[:], OP.is_equal, ["jk", "kk"], "mk2")
+        R(i, 4 + i, "big", T0, NT, "hr0", NT, ["bt"])
+    pick_c("ur2", 0, 128, "uq", 0, 2, "z16", 0, ["uq", "z16"], "ur2")
+    pick_s("ur2", 0, 128, "uq", 0, 2, "z16", 0, ["uq", "z16"], "ur2s")
     quant("w2", 0, 128, T.w2b[:], hk("w2b"), "w2")
-    V(lambda e: e.tensor_scalar(T.thr[:], T.mk2[:], -400.0, CH - 7.5 + 400.0, OP.mult, OP.add), ["mk2"], ["thr"])
     for i in range(4):
         add(i, i, "hx", CH, NT, "hr0", "h0")
         if i == 0:
-            pick_c("ur2", 0, 128, "uq", 0, 2, "z16", 0, ["uq", "z16"], "ur2")
-            pick_s("ur2", 0, 128, "uq", 0, 2, "z16", 0, ["uq", "z16"], "ur2s")
             quant("wq", 0, 128, T.wb[:], ["wb"], "wq")
-            ycopy(4, T0, NT, ["bt", "bts"])
+            ycopy(4, T0, NT, ["bt"])
     quant("big", CH, HALF, T.hx[:, 4 * CH:4 * HALF], hk("h0"), "bh0")
     cp(T.lif[:, 0:6], T.lin[:], ["lin"], "lif1")
-    cp(T.off1f[:], T.off1[:], ["off1"], "off1f")
     stores = [0]
 
     def store(q, pairs, reads):
@@ -379,11 +372,12 @@ def rank_program(g, core, T, topo):
         stores[0] += 16 * len(pairs)
     store("Y", [(T.li[0:1, 16 * k:16 * k + 16], T.lif[0:16, k:k + 1]) for k in range(6)], ["lif1"])
 
-    mk = ["bt", "bts", "bm", "bms"]
+    mk = ["bt", "bm"]
     for c in range(3):
         pick_c("t1", 128 * c, 128, "big", HALF, 2 * HALF, "off1", 8 * c, mk + ["off1"], "t1c%d" % c)
         pick_s("t1", 128 * c, 128, "big", HALF, 2 * HALF, "off1", 8 * c, mk + ["off1"], "t1s%d" % c)
-        scores(c, "t1", "ur2", ["t1c%d" % c, "t1s%d" % c, "ur2", "ur2s"], "cr")
+        scores(c, "t1", "ur2", ["t1c%d" % c, "t1s%d" % c, "ur2", "ur2s"])
+    cp(T.off1f[:], T.off1[:], ["off1"], "off1f")
 
     def N(what, i, bank):
         if what == "D":
@@ -395,20 +389,20 @@ def rank_program(g, core, T, topo):
         if c == 0:
             N("D", 0, 2), N("R", 0, 1), N("D", 1, 3)
         elif c == 1:
-            N("R", 1, 5), N("R", 2, 1)
+            N("R", 1, 5)
         elif c == 2:
-            N("R", 3, 5), N("D", 2, 0)
+            N("R", 2, 1), N("R", 3, 5), N("D", 2, 0)
         else:
             N("D", 3, 6)
     order(beside)
     add(0, 2, "hx", 0, CH, "hr1", "h1")
     add(1, 3, "hx", 0, CH, "hr1", "h1")
     for t in range(3):
-        V(lambda e, t=t: e.tensor_scalar(T.xo2[:, t:96:4], T.thr[:, t:96:4], B(4, t, t + 1), float(HALF), OP.is_le, OP.mult),
-          ["thr", "b4", "xo2z"], ["xo2%d" % t])
-    quant("xo2q", 0, 128, T.xo2[:], ["xo2z", "xo20", "xo21", "xo22"], "xo2q")
+        V(lambda e, t=t: e.tensor_scalar(T.xo[:, t:96:4], T.thr[:, t:96:4], B(4, t, t + 1), float(HALF), OP.is_le, OP.mult),
+          ["thr", "b4", "xoz", "xoq"], ["xo2%d" % t])
+    quant("xoq", 0, 128, T.xo[:, 0:512], ["xoz"] + hk("xo2", 3), "xoq")
     ycopy(2, 128, HALF - 128, ["bh0"])
-    mm(1, 128, "w2", 0, "xo2q", 0, True, True, ["xo2q", "w2"])
+    mm(1, 128, "w2", 0, "xoq", 0, True, True, ["xoq", "w2"])
     ycopy(3, HALF, CH, mk)
     add(2, 0, "hx", 0, CH, "hr1", "h1")
     add(3, 6, "hx", 0, CH, "hr1", "h1")
@@ -418,26 +412,20 @@ def rank_program(g, core, T, topo):
     cp(T.off2[:], T.off2f[:], ["off2f"], "off2")
     al = ["bh0", "bh1", "off2"] + mk
     yk = ["yw%d" % a for a in (0, 128, HALF, T0)]
-
-    def pick_y(q, a, b, key):
-        src = T.yw[:].indirect(T.off2[:, a // 16:b // 16])
-        if q == "V":
-            cp(T.yb[:, a:b], src, yk + ["off2"], key)
-        else:
-            S(lambda e: e.activation(T.yb[:, a:b], src, AF.Copy), yk + ["off2"], [key])
     for c in range(3):
         pick_c("oq", 128 * c, 128, "big", 0, 2 * HALF, "off2", 8 * c, al, "oq%d" % c)
         store("Y", [(T.oc[:, 512 * c:512 * c + 512], u8("oq", 128 * c, 128 * c + 128))], ["oq%d" % c])
-    pick_y("S", 0, 192, "yb0")
-    store("Y", [(T.y[:, 0:192], T.yb[:, 0:192])], ["yb0"])
+    for a in (0, 192):
+        S(lambda e, a=a: e.activation(T.yb[:, a:a + 192], T.yw[:].indirect(T.off2[:, a // 16:a // 16 + 12]), AF.Copy),
+          yk + ["off2"], ["yb%d" % a])
+        store("Y", [(T.y[:, a:a + 192], T.yb[:, a:a + 192])], ["yb%d" % a])
     pick_s("oq", 0, NT, "big", 0, 2 * HALF, "off2", 0, al, "oqs")
     store("S", [(T.osc[4 * k:4 * k + 4, :], T.oqs[32 * k:32 * k + 4, :]) for k in range(4)], ["oqs"])
-    pick_y("V", 192, 384, "yb1")
-    store("Y", [(T.y[:, 192:384], T.yb[:, 192:384])], ["yb1"])
     onehot()
     list_mm(7)
     cp(T.lif[:, 6:12], B(7, 0, 6), ["b7"], "lif2")
-    store("Y", [(T.li[1:2, 16 * k:16 * k + 16], T.lif[0:16, 6 + k:7 + k]) for k in range(6)], ["lif2"])
+    for q, ks in (("Y", (0, 1, 2)), ("S", (3, 4, 5))):
+        store(q, [(T.li[1:2, 16 * k:16 * k + 16], T.lif[0:16, 6 + k:7 + k]) for k in ks], ["lif2"])
 
     for q in ("V", "T", "S", "G"):
         g.wait_ge(T.sem["s" + q], cnt[q])

@@ -23,13 +23,15 @@ def codes(**names):
 SCRATCH = {
     "ps": ("psum", [128, 4096], "float32"),
     "ub": sb(512, "bfloat16"), "xb": sb(4 * NT, "bfloat16"), "vb": sb(2048, "bfloat16"), "wb": sb(512, "bfloat16"),
-    "ones": sb(128, "bfloat16"), "z16": sb(8, "uint16"), "eb": sb(520, "bfloat16"), "zi": sb(256, "bfloat16"),
+    "ones": sb(128, "bfloat16"), "zz": sb(560, "bfloat16"), "z16": sb(8, "uint16"), "eb": sb(520, "bfloat16"),
+    "zi": sb(256, "bfloat16"), "zj": sb(256, "bfloat16"),
     "tri": sb(128, "bfloat16"), "q0": sb(128, "bfloat16"), "qm": sb(128, "bfloat16"), "pp": sb(128, "bfloat16"),
-    "kc": sb(48, "float32"), "jj": sb(96, "int32"), "kk": sb(96, "int32"), "j16": sb(96, "int32"),
-    "ja": sb(96, "int32"), "jb": sb(96, "int32"), "jk": sb(96, "int32"), "g3": sb(16, "int32"), "g3a": sb(16, "int32"),
+    "pm": sb(128, "bfloat16"), "wa": sb(128, "bfloat16"),
+    "kc": sb(48, "float32"), "jj": sb(24, "int32"), "kk": sb(16, "int32"), "j16": sb(24, "int32"),
+    "ja": sb(24, "int32"), "jb": sb(24, "int32"), "jk": sb(16, "int32"), "g3": sb(16, "int32"), "g3a": sb(16, "int32"),
     "g3b": sb(16, "int32"), "i3": sb(16, "int32"), "p16": sb(4, "int32"), "p128": sb(4, "int32"),
     "p16f": sb(4, "float32"), "s4": sb(4, "float32"), "ab": sb(48, "float32"), "ab2": sb(8, "float32"),
-    "mk1": sb(16, "bfloat16"), "mk2": sb(96, "float32"), "thr": sb(96, "float32"),
+    "mk1": sb(16, "bfloat16"), "c88": sb(96, "float32"), "tha": sb(96, "float32"), "thr": sb(96, "float32"),
     "w1b": sb(512, "bfloat16"), "w2b": sb(512, "bfloat16"), "zb": sb(768, "bfloat16"),
     "sc": sb(3, "float32"), "dl": sb(3, "float32"), "mt": sb(NT, "float32"), "cmp": sb(4 * NT, "bfloat16"),
     "kl": sb(52, "float32"), "x0": sb(48, "float32"), "wx": sb(560, "bfloat16"),
@@ -39,19 +41,21 @@ SCRATCH = {
     "lin": sb(6, "uint16"), "offd": ("dram", [128, 3], "uint16"), "off1": sb(24, "uint16"), "off1f": sb(24, "float32"),
     "hrb": sb(4 * CH, "float32"), "hr0": sb(4 * NT, "float32"), "hr1": sb(4 * CH, "float32"),
     "hb": sb(512, "bfloat16"), "hx": sb(4 * HALF, "bfloat16"),
-    "yb": sb(NT, "float32"), "yw": sb(2 * HALF, "float32"), "lif": sb(12, "float32"),
+    "yb": sb(NT, "float32"), "lif": sb(6, "float32"), "lir": sb(96, "float32"),
 }
 SCRATCH.update(codes(uq=128, ur1=128, ur2=128, t0=NT, vq=512, wq=128, qe=CH + 512, w1=128, w2=128, zq=192, cq=NT, wxq=140,
                      xoq=136, q1=CH, m1=128, big=2 * HALF, t1=NT, oq=NT))
 SCRATCH.update({"uin": sb(2, F8), "uins": sb(8, "uint8")})
 SEMAPHORES = ["sV", "sT", "sS", "sG", "du", "dx0", "dx1", "dx2", "dv0", "dv1", "dv2", "dv3", "dw", "doff", "dst",
-              "au", "aq", "at", "am", "al", "ao", "ls"]
+              "au", "aq", "at", "am", "al", "ao", "go", "ls"]
 
 OP = AluOpType
 AF = ActivationFunctionType
 BIG16 = 201326592.0
 ULP = 1.03125 * 2.0 ** -24
 TINY = 1e-37
+C05 = 13421773 * 2.0 ** -28
+BANKS = ["b%d" % k for k in range(8)]
 
 
 def sched(g, T):
@@ -64,6 +68,10 @@ def sched(g, T):
         for k in reads:
             for qq, s, v in wr.get(k, []):
                 req[s] = max(req.get(s, 0), v)
+            if k in BANKS:
+                for qq, s, v in rd.get(k, []):
+                    if qq != q:
+                        req[s] = max(req.get(s, 0), v)
         for k in writes:
             for qq, s, v in wr.get(k, []) + rd.get(k, []):
                 if qq != q or q != "T":
@@ -126,10 +134,11 @@ def rank_program(g, core, T, topo):
 
     arrive("au", 8, ["uin", "uins"])
     arrive("aq", 32, ["qin"])
-    arrive("at", 16, ["bt"])
+    arrive("at", 32, ["bt"])
     arrive("am", 32, ["bm"])
     arrive("al", 8, ["lin"])
     arrive("ao", 8, ["offd"])
+    arrive("go", 1, ["go"])
 
     def V(f, reads, writes):
         op("V", f, reads, writes)
@@ -154,6 +163,12 @@ def rank_program(g, core, T, topo):
 
     def cp(out, in_, reads, key):
         V(lambda e: e.tensor_copy(out, in_), reads, [key])
+
+    def act(out, in_, f, bias, scale, reads, key):
+        S(lambda e: e.activation(out, in_, f, bias=bias, scale=scale), reads, [key])
+
+    def zero(out, w, key):
+        S(lambda e: e.activation(out, T.zz[:, 0:w], AF.Copy), ["zz"], [key])
 
     def quant(out, a, b, src, reads, key):
         V(lambda e: e.quantize_mx(T[out][:, a:b], T[out + "s"][:, a:b], src), reads, [key])
@@ -181,19 +196,12 @@ def rank_program(g, core, T, topo):
         dma("Y", [(T.xb[:, 512 * c:512 * c + 512], T.x[:, 512 * c:512 * c + 512])], "dx%d" % c, 16, [], ["xb%d" % c])
 
     memset(T.ub[:, 8:512], 0.0, "ubz")
-    memset(T.ones[:], 1.0, "ones")
-    G(lambda e: e.iota(T.jj[:], [[0, 24], [128, 4]], 0, 1), [], ["jj"])
-    G(lambda e: e.iota(T.kk[:], [[1, 24], [0, 4]], 0, 0), [], ["kk"])
+    memset(T.zz[:], 0.0, "zz")
+    G(lambda e: e.iota(T.jj[:], [[0, 6], [128, 4]], 0, 1), [], ["jj"])
     iota(T.zi[:], [[0, 16], [1, 4], [0, 4]], "zi")
-    G(lambda e: e.affine_select(T.tri[:], T.ones[:], [[1, 128]], OP.is_gt, 0.0, 0, -1), ["ones"], ["tri"])
+    memset(T.ones[:], 1.0, "ones")
+    memset(T.eb[:], 0.0, "ebz")
     memset(T.z16[:], 0, "z16")
-    memset(T.eb[:], 0.0, "eb")
-    ts(T.j16[:], T.jj[:], 16, OP.add, ["jj"], "j16")
-    ts(T.jk[:], T.jj[:], 4, OP.logical_shift_right, ["jj"], "jk")
-    ts(T.p16[:], T.jj[:, 0:4], 15, OP.bitwise_and, ["jj"], "p16")
-    ts(T.ja[:], T.j16[:], 480, OP.bitwise_and, ["j16"], "ja")
-    ts(T.g3a[:], T.jk[:, 0:16], 11, OP.mult, ["jk"], "g3a")
-    ts(T.p128[:], T.p16[:], 8, OP.mult, ["p16"], "p128")
     quant("uq", 0, 128, T.ub[:], ["ub", "ubz"], "uq")
     wait("G", ["uq"], [])
     rid, pid, _ = topo.addr(prv)
@@ -203,87 +211,100 @@ def rank_program(g, core, T, topo):
                         RemoteDMATransfer(dst_ids=[DstId(rid=rid, pnc=pid)], dma_engine_mask=bits(e0[4:]), remote_sem=T.sem["au"],
                                           src=T.uqs[:, 0:8], dst=T.uins[:, 0:8])], local_sem=T.sem["ls"])
     loc[0] += len(e0)
-    G(lambda e: e.affine_select(T.eb[:, 4:516:4], T.ones[:], [[-1, 128]], OP.is_equal, 0.0, 0, 1), ["ones", "eb"], ["ebi"])
+    G(lambda e: e.affine_select(T.eb[:, 4:516:4], T.ones[:], [[-1, 128]], OP.is_equal, 0.0, 0, 1), ["ones", "ebz"], ["ebi"])
+    G(lambda e: e.iota(T.kk[:], [[1, 4], [0, 4]], 0, 0), [], ["kk"])
+    G(lambda e: e.affine_select(T.tri[:], T.ones[:], [[1, 128]], OP.is_gt, 0.0, 0, -1), ["ones"], ["tri"])
+    iota(T.q0[:], [[0, 8], [1, 16]], "q0")
     iota(T.pp[:], [[1, 128]], "pp")
+    zero(T.wx[:], 560, "wxz")
+    act(T.zb[:, 0:256], T.zi[:], AF.Relu, 1.0, -1.0, ["zi"], "zb0")
+    act(T.zj[:], T.zi[:], AF.Abs, -1.0, 1.0, ["zi"], "zj")
+    zero(T.zb[:, 512:768], 256, "zb2")
+    act(T.zb[:, 256:512], T.zj[:], AF.Relu, 1.0, -1.0, ["zj"], "zb1")
+    ts(T.j16[:], T.jj[:], 16, OP.add, ["jj"], "j16")
+    ts(T.jk[:], T.jj[:, 0:16], 4, OP.logical_shift_right, ["jj"], "jk")
+    ts(T.p16[:], T.jj[:, 0:4], 15, OP.bitwise_and, ["jj"], "p16")
+    ts(T.ja[:], T.j16[:], 480, OP.bitwise_and, ["j16"], "ja")
+    ts(T.g3a[:], T.jk[:], 11, OP.mult, ["jk"], "g3a")
+    ts(T.p128[:], T.p16[:], 8, OP.mult, ["p16"], "p128")
     tt(T.jb[:], T.jj[:], T.ja[:], OP.subtract, ["jj", "ja"], "jb")
     ts(T.g3[:], T.g3a[:], 5, OP.logical_shift_right, ["g3a"], "g3")
+    cp(T.ab[:, 0:24], T.ja[:], ["ja"], "aba")
+    cp(T.ab[:, 24:48], T.jb[:], ["jb"], "abb")
     cp(T.p16f[:], T.p16[:], ["p16"], "p16f")
-    cp(T.ab[:, 0:24], T.ja[:, 0:24], ["ja"], "aba")
-    ts(T.ab2[:, 0:4], T.ja[:, 0:4], float(CH), OP.add, ["ja"], "ab2a")
-    ts(T.g3b[:], T.g3[:], 3, OP.mult, ["g3"], "g3b")
     tt(T.s4[:], T.p128[:], T.g3[:, 0:4], OP.add, ["p128", "g3"], "s4")
-    cp(T.ab[:, 24:48], T.jb[:, 0:24], ["jb"], "abb")
-    cp(T.ab2[:, 4:8], T.jb[:, 0:4], ["jb"], "ab2b")
-    tt(T.i3[:], T.jk[:, 0:16], T.g3b[:], OP.subtract, ["jk", "g3b"], "i3")
-    for k in range(2):
-        ts(T.zb[:, 256 * k:256 * k + 256], T.zi[:], float(k), OP.is_equal, ["zi"], "zb%d" % k)
-    memset(T.zb[:, 512:768], 0.0, "zb2")
-    memset(T.ab[:, 3:48:4], 0.0, "ab", ["aba", "abb"])
-    tt(T.mk1[:], T.i3[:], T.kk[:, 0:16], OP.is_equal, ["i3", "kk"], "mk1a")
-    memset(T.wx[:], 0.0, "wxz")
-    memset(T.mk1[:, 3:16:4], 0.0, "mk1", ["mk1a"])
     for c in range(3):
         quant("t0", 128 * c, 128 * c + 128, T.xb[:, 512 * c:512 * c + 512], ["xb%d" % c], "t0%d" % c)
+        if c < 2:
+            for b in (2 * c, 2 * c + 1):
+                quant("qe", CH + 128 * b, CH + 128 * b + 128, T.eb[:, 4 - b:516 - b], ["ebz", "ebi"], "eq%d" % b)
     t0 = hk("t0", 3)
-    send(nx2, u8("big", T0, T0 + NT), u8("t0", 0, NT), "at", half(nx2, 1), t0)
-    send(nx2, T.bigs[:, T0:T0 + NT], T.t0s[:, 0:NT], "at", half(nx2, 1), [])
+    send(nx2, u8("big", T0, T0 + NT), u8("t0", 0, NT), "at", topo.engines(core, nx2), t0)
+    send(nx2, T.bigs[:, T0:T0 + NT], T.t0s[:, 0:NT], "at", topo.engines(core, nx2), [])
+    g.sem_inc(T.sem["go"], 1)
+    for i in range(4):
+        dma("Y", [(T.vb[:, 512 * i:512 * i + 512], T.v[:, 512 * i:512 * i + 512])], "dv%d" % i, 16, ["go", "uin"], ["vb%d" % i])
     for c in range(3):
-        G(lambda e, c=c: e.affine_select(T.cmp[:, 512 * c + c:512 * c + 512:4], T.wx[:, 0:128], [[0, 128]], OP.not_equal, -7.5, 0, 1),
-          ["wxz"], ["cm%d%d" % (c, c)])
+        G(lambda e, c=c: e.affine_select(T.cmp[:, 512 * c + c:512 * c + 512:4], T.zz[:, 0:128], [[0, 128]], OP.not_equal, -7.5, 0, 1),
+          ["zz"], ["cm%d%d" % (c, c)])
     iota(T.kc[:], [[0, 2], [16, 6], [0, 4]], "kc")
-    iota(T.q0[:], [[0, 8], [1, 16]], "q0")
-    iota(T.xo[:], [[0, 544]], "xoz")
-    quant("zq", 0, 192, T.zb[:], hk("zb", 3), "zq")
-    for b in range(4):
-        quant("qe", CH + 128 * b, CH + 128 * b + 128, T.eb[:, 4 - b:516 - b], ["eb", "ebi"], "eq%d" % b)
+    cp(T.zb[:, 752:755], T.jb[:, 0:3], ["jb", "zb2"], "zba")
+    cp(T.zb[:, 760:763], T.ja[:, 0:3], ["ja", "zb2"], "zbb")
+    memset(T.ab[:, 3:48:4], 0.0, "ab", ["aba", "abb"])
+    quant("zq", 0, 192, T.zb[:], hk("zb", 3) + ["zba", "zbb"], "zq")
     pick_c("ur1", 0, 128, "uin", 0, 2, "z16", 0, ["uin", "uins", "z16"], "ur1")
     pick_s("ur1", 0, 128, "uin", 0, 2, "z16", 0, ["uin", "uins", "z16"], "ur1s")
     for t in range(4):
         ts(T.w1b[:, t:512:4], T.pp[:], T.s4[:, t:t + 1], OP.is_equal, ["pp", "s4"], "w1b%d" % t)
+    ts(T.g3b[:], T.g3[:], 3, OP.mult, ["g3"], "g3b")
+    ts(T.ab2[:, 0:4], T.ja[:, 0:4], float(CH), OP.add, ["ja"], "ab2a")
+    act(T.qm[:], T.q0[:], AF.Identity, -7.5, 1.0, ["q0"], "qm")
+    act(T.wa[:], T.q0[:], AF.Abs, T.p16f[:, 0:1], -1.0, ["q0", "p16f"], "wa")
+    for t in range(2):
+        act(T.w2b[:, t:512:4], T.wa[:], AF.Relu, 1.0, -1.0, ["wa"], "w2b%d" % t)
 
     ROW = (0, 6, 7)
 
-    def scores(c, tok, ur, keys):
+    def col(c, tok, ur, keys):
         mm(1 + c, 128, tok, 128 * c, ur, 0, True, True, keys)
+
+    def row(c, tok, ur, keys):
         mm(ROW[c], 128, ur, 0, tok, 128 * c, True, True, keys)
 
-    def order(beside):
-        def against(c, t, col, key):
-            ts(T.cmp[:, 512 * c + t:512 * c + 512:4], B(ROW[c], 0, 128), col, OP.is_le if t < c else OP.is_lt,
-               ["b%d" % ROW[c], key], "cm%d%d" % (c, t))
-        against(0, 1, B(2, 0, 1), "b2"), against(1, 0, B(1, 0, 1), "b1")
+    def order(beside, early):
+        def against(c, t):
+            ts(T.cmp[:, 512 * c + t:512 * c + 512:4], B(ROW[c], 0, 128), B(1 + t, 0, 1), OP.is_le if t < c else OP.is_lt,
+               ["b%d" % ROW[c], "b%d" % (1 + t)], "cm%d%d" % (c, t))
+        against(0, 1)
+        if not early:
+            against(1, 0)
         cp(T.sc[:], ps[:, 512:2048:512], ["b1", "b2", "b3"], "sc")
-        S(lambda e: e.activation(T.dl[:], T.sc[:], AF.Abs, bias=TINY, scale=ULP), ["sc"], ["dl"])
-        for c, t in ((0, 2), (1, 2), (2, 0), (2, 1)):
-            against(c, t, T.sc[:, t:t + 1], "sc")
+        act(T.dl[:], T.sc[:], AF.Abs, TINY, ULP, ["sc"], "dl")
+        for c, t in ((0, 2),) + ((1, 0),) * early + ((1, 2), (2, 0), (2, 1)):
+            against(c, t)
         for c in range(3):
-            S(lambda e, c=c: e.activation(T.mt[:, 128 * c:128 * c + 128], T.tri[:], AF.Identity, bias=T.sc[:, c:c + 1],
-                                          scale=T.dl[:, c:c + 1]), ["tri", "sc", "dl"], ["mt%d" % c])
+            act(T.mt[:, 128 * c:128 * c + 128], T.tri[:], AF.Identity, T.sc[:, c:c + 1], T.dl[:, c:c + 1],
+                ["tri", "sc", "dl"], "mt%d" % c)
+
+        def diagonal(c):
             tt(T.cmp[:, 512 * c + 3:512 * c + 512:4], B(ROW[c], 0, 128), T.mt[:, 128 * c:128 * c + 128], OP.is_lt,
                ["b%d" % ROW[c], "mt%d" % c], "cm%d3" % c)
+
+        def pack(c):
             quant("cq", 128 * c, 128 * c + 128, T.cmp[:, 512 * c:512 * c + 512], hk("cm%d" % c), "cq%d" % c)
             beside(c)
+        diagonal(0), diagonal(1), pack(0), diagonal(2), pack(1), pack(2)
         for c in range(3):
             mm(4, 128, "cq", 128 * c, "zq", (0, 64, 2)[c], c == 0, c == 2, ["cq%d" % c, "zq"])
-            if c == 0:
-                beside(3)
+        beside(3)
 
-    def onehot():
-        V(lambda e: e.tensor_scalar(T.kl[:, 0:48], B(4, 0, 48), BIG16, BIG16, OP.add, OP.subtract), ["b4"], ["kl"])
-        tt(T.x0[:], T.kl[:, 0:48], T.kc[:], OP.is_equal, ["kl", "kc"], "x0")
-        for t in range(3):
-            V(lambda e, t=t: e.tensor_scalar(T.wx[:, 48 + t:560:4], T.qm[:], T.kl[:, t:t + 1], B(4, t, t + 1), OP.add, OP.is_equal),
-              ["kl", "qm", "b4", "wxz"], ["wx%d" % t])
-        tt(T.wx[:, 0:48], T.x0[:], T.ab[:], OP.mult, ["x0", "ab", "wxz", "cm00", "cm11", "cm22"], "wxx")
-        quant("wxq", 0, 140, T.wx[:], ["wxz", "wx0", "wx1", "wx2", "wxx"], "wxq")
-
-    def list_mm(bank):
-        mm(bank, 128, "wxq", 12, "wxq", 0, True, False, ["wxq"])
-        mm(bank, 128, "wxq", 12, "wxq", 6, False, True, ["wxq"])
-
-    def R(i, bank, q, q0, w, out, w2, keys):
+    def R(i, bank, q, q0, w, out, w2, keys, by="S"):
         mm(bank, w, "vq", 128 * i, q, q0, True, True, keys + ["vq%d" % i])
-        S(lambda e: e.activation(T[out][:, w2 * i:w2 * i + w2], B(bank, 0, w2), AF.Relu, scale=0.05), ["b%d" % bank], [out + str(i)])
+        o = T[out][:, w2 * i:w2 * i + w2]
+        if by == "S":
+            S(lambda e: e.activation(o, B(bank, 0, w2), AF.Relu, scale=0.05), ["b%d" % bank], [out + str(i)])
+        else:
+            V(lambda e: e.tensor_scalar(o, B(bank, 0, w2), 0.0, C05, OP.max, OP.mult), ["b%d" % bank], [out + str(i)])
 
     def D(i, bank, q, q0, w, keys):
         mm(bank, w, "qe", CH + 128 * i, q, q0, True, True, keys + ["eq%d" % i])
@@ -291,93 +312,104 @@ def rank_program(g, core, T, topo):
     def add(i, bank, h, c0, w, hr, key):
         tt(T[h][:, 4 * c0 + i:4 * (c0 + w):4], T[hr][:, w * i:w * i + w], B(bank, 0, w), OP.add, [hr + str(i), "b%d" % bank], key + str(i))
 
-    def ycopy(bank, a, w, reads):
-        mm(bank, max(w, 128), "wq", 0, "big", a, True, True, ["wq"] + reads)
-        S(lambda e: e.activation(T.yw[:, a:a + w], B(bank, 0, w), AF.Copy), ["b%d" % bank], ["yw%d" % a])
+    def D0(b):
+        D(b, b, "big", T0, NT, ["bt"])
 
-    for c in range(3):
-        scores(c, "t0", "ur1", ["t0%d" % c, "ur1", "ur1s"])
-    order(lambda c: None)
-    for i in range(4):
-        dma("Y", [(T.vb[:, 512 * i:512 * i + 512], T.v[:, 512 * i:512 * i + 512])], "dv%d" % i, 16, ["sc"], ["vb%d" % i])
-    ts(T.qm[:], T.q0[:], -7.5, OP.add, ["q0"], "qm")
-    memset(T.hb[:, 4 * CH:512], 0.0, "hbz")
-    onehot()
-    list_mm(5)
-    ts(T.rkp[:], B(4, 0, 4), 7.5, OP.add, ["b4"], "rkp")
+    def R0(i, bank):
+        R(i, bank, "big", T0, NT, "hr0", NT, ["bt"])
+
+    def A0(i):
+        add(i, i, "hx", CH, NT, "hr0", "h0")
+
+    def VQ(i):
+        quant("vq", 128 * i, 128 * i + 128, T.vb[:, 512 * i:512 * i + 512], ["vb%d" % i], "vq%d" % i)
+
+    for f, c in ((row, 0), (col, 1), (col, 0), (col, 2), (row, 1), (row, 2)):
+        f(c, "t0", "ur1", ["t0%d" % c, "ur1", "ur1s"])
+    order(lambda c: None, 1)
+    zero(T.xo[:], 544, "xoz")
+    for t in range(2, 4):
+        act(T.w2b[:, t:512:4], T.wa[:], AF.Relu, 1.0, -1.0, ["wa"], "w2b%d" % t)
+    quant("w1", 0, 128, T.w1b[:], hk("w1b"), "w1")
+    tt(T.i3[:], T.jk[:], T.g3b[:], OP.subtract, ["jk", "g3b"], "i3")
+    cp(T.ab2[:, 4:8], T.jb[:, 0:4], ["jb"], "ab2b")
+    V(lambda e: e.tensor_scalar(T.kl[:, 0:48], B(4, 0, 48), BIG16, BIG16, OP.add, OP.subtract), ["b4"], ["kl"])
     ts(T.sel[:], B(4, 0, 8), CH - 7.5, OP.is_lt, ["b4"], "sel")
+    tt(T.x0[:], T.kl[:, 0:48], T.kc[:], OP.is_equal, ["kl", "kc"], "x0")
+    for t in range(3):
+        V(lambda e, t=t: e.tensor_scalar(T.wx[:, 48 + t:560:4], T.qm[:], T.kl[:, t:t + 1], B(4, t, t + 1), OP.add, OP.is_equal),
+          ["kl", "qm", "b4", "wxz"], ["wx%d" % t])
+        if t == 1:
+            tt(T.wx[:, 0:48], T.x0[:], T.ab[:], OP.mult, ["x0", "ab", "wxz"], "wxx")
+    ts(T.rkp[:], B(4, 0, 4), 7.5, OP.add, ["b4"], "rkp")
+    quant("wxq", 0, 140, T.wx[:], ["wxz", "wx0", "wx1", "wx2", "wxx"], "wxq")
+    mm(5, 128, "wxq", 12, "wxq", 0, True, False, ["wxq"])
+    mm(5, 128, "wxq", 12, "wxq", 6, False, True, ["wxq"])
+    tt(T.mk1[:], T.i3[:], T.kk[:], OP.is_equal, ["i3", "kk"], "mk1a")
     tt(T.kl[:, 48:52], T.rkp[:], T.kl[:, 44:48], OP.subtract, ["rkp", "kl"], "kl2")
-    tt(T.hl[:], T.kl[:, 44:52], T.ab2[:], OP.subtract, ["kl", "kl2", "ab2a", "ab2b"], "hl")
+    memset(T.mk1[:, 3:16:4], 0.0, "mk1", ["mk1a"])
     cp(T.lst1[:], B(5, 0, 6), ["b5"], "lst1")
+    tt(T.hl[:], T.kl[:, 44:52], T.ab2[:], OP.subtract, ["kl", "kl2", "ab2a", "ab2b"], "hl")
     pick_c("q1", 0, CH, "t0", 0, NT, "lst1", 0, t0 + ["lst1"], "q1")
     pick_s("q1", 0, CH, "t0", 0, NT, "lst1", 0, t0 + ["lst1"], "q1s")
     send(nxt, u8("qe", 0, CH), u8("q1", 0, CH), "aq", topo.engines(core, nxt), ["q1"])
     send(nxt, T.qes[:, 0:CH], T.q1s[:, 0:CH], "aq", topo.engines(core, nxt), ["q1s"])
     tt(T.hm[:], T.hl[:], T.sel[:], OP.mult, ["hl", "sel"], "hm")
-    quant("w1", 0, 128, T.w1b[:], hk("w1b"), "w1")
+    quant("w2", 0, 128, T.w2b[:], hk("w2b"), "w2")
     tt(T.hn[:], T.hm[:], T.ab2[:], OP.add, ["hm", "ab2a", "ab2b"], "hn")
     for k in range(2):
         for t in range(3):
             ts(T.xo[:, 16 * k + t:16 * k + 16:4], T.mk1[:, t:16:4], T.hn[:, 4 * k + t:4 * k + t + 1], OP.mult,
                ["hn", "mk1", "xoz"], "xo%d%d" % (k, t))
     quant("xoq", 0, 136, T.xo[:], ["xoz"] + hk("xo0", 3) + hk("xo1", 3), "xoq")
-
-    def D0(b):
-        D(b, b, "big", T0, NT, ["bt"])
-    D0(0), D0(1)
+    act(T.c88[:], T.ones[:, 0:96], AF.Identity, CH - 7.5, 0.0, ["ones"], "c88")
+    act(T.pm[:], T.pp[:], AF.Identity, -7.5, 1.0, ["pp"], "pm")
+    zero(T.hb[:, 4 * CH:512], 128, "hbz")
+    pick_s("ur2", 0, 128, "uq", 0, 2, "z16", 0, ["uq", "z16"], "ur2s")
+    G(lambda e: e.affine_select(T.tha[:], T.c88[:], [[-16, 24], [128, 4]], OP.is_ge, CH + 392.5, 0, 1), ["c88"], ["tha"])
+    G(lambda e: e.affine_select(T.thr[:], T.tha[:], [[16, 24], [-128, 4]], OP.is_ge, CH + 392.5, 15, -1), ["tha"], ["thr"])
+    D0(0), D0(1), D0(2)
     mm(6, 128, "w1", 0, "xoq", 0, True, False, ["xoq", "w1"])
     mm(6, 128, "w1", 0, "xoq", 4, False, True, ["xoq", "w1"])
-    D0(2), D0(3)
-    tt(T.mk2[:], T.jk[:], T.kk[:], OP.is_equal, ["jk", "kk"], "mk2")
-    for t in range(4):
-        ts(T.w2b[:, t:512:4], T.q0[:], T.p16f[:, t:t + 1], OP.is_equal, ["q0", "p16f"], "w2b%d" % t)
+    VQ(0), VQ(1)
     cp(T.offc[:], B(6, 0, 3), ["b6"], "offc")
     send(nx2, T.offd[:], T.offc[:], "ao", half(nx2, 0), ["offc"])
     send(nx2, T.lin[:], T.lst1[:], "al", half(nx2, 0), ["lst1"])
-    for i in range(4):
-        quant("vq", 128 * i, 128 * i + 128, T.vb[:, 512 * i:512 * i + 512], ["vb%d" % i], "vq%d" % i)
-    V(lambda e: e.tensor_scalar(T.thr[:], T.mk2[:], -400.0, CH - 7.5 + 400.0, OP.mult, OP.add), ["mk2"], ["thr"])
+    VQ(2), VQ(3)
+    pick_c("ur2", 0, 128, "uq", 0, 2, "z16", 0, ["uq", "z16"], "ur2")
+    R0(0, 7)
 
-    def RB(i, bank):
-        R(i, bank, "qe", 0, 128, "hrb", CH, ["qin", "eq0"])
+    def RB(i, bank, by):
+        R(i, bank, "qe", 0, 128, "hrb", CH, ["qin", "eq0"], by)
 
     def DB(i, bank):
         D(i, bank, "qe", 0, 128, ["qin", "eq0"])
 
     def AB(i, bank):
         add(i, bank, "hb", 0, CH, "hrb", "hb")
-    RB(0, 4), RB(1, 5), DB(0, 6), RB(2, 4), DB(1, 7), RB(3, 5)
-    AB(0, 6), DB(2, 6), AB(1, 7), DB(3, 7), AB(2, 6), AB(3, 7)
+    RB(0, 4, "V"), RB(1, 5, "S"), RB(2, 3, "V"), DB(0, 6), RB(3, 4, "S"), DB(2, 7), DB(1, 5), DB(3, 3)
+    AB(0, 6), AB(2, 7), AB(1, 5), AB(3, 3)
     quant("m1", 0, 128, T.hb[:], ["hbz"] + hk("hb"), "m1")
     send(nxt, u8("big", HALF, HALF + CH), u8("m1", 0, CH), "am", topo.engines(core, nxt), ["m1"])
     send(nxt, T.bigs[:, HALF:HALF + CH], T.m1s[:, 0:CH], "am", topo.engines(core, nxt), [])
     dma("Y", [(T.wb[:], T.w[:])], "dw", 16, ["qin"], ["wb"])
     dma("Y", [(T.off1[16 * h:16 * h + 16, :], T.offd[:]) for h in range(8)], "doff", 128, ["offd"], ["off1"])
+    R0(1, 4), R0(2, 6), D0(3), R0(3, 7)
     for i in range(4):
-        R(i, 4 + i, "big", T0, NT, "hr0", NT, ["bt"])
-    pick_c("ur2", 0, 128, "uq", 0, 2, "z16", 0, ["uq", "z16"], "ur2")
-    pick_s("ur2", 0, 128, "uq", 0, 2, "z16", 0, ["uq", "z16"], "ur2s")
-    quant("w2", 0, 128, T.w2b[:], hk("w2b"), "w2")
-    for i in range(4):
-        add(i, i, "hx", CH, NT, "hr0", "h0")
-        if i == 0:
-            quant("wq", 0, 128, T.wb[:], ["wb"], "wq")
-            ycopy(4, T0, NT, ["bt"])
-    quant("big", CH, HALF, T.hx[:, 4 * CH:4 * HALF], hk("h0"), "bh0")
-    cp(T.lif[:, 0:6], T.lin[:], ["lin"], "lif1")
+        A0(i)
+    quant("wq", 0, 128, T.wb[:], ["wb"], "wq")
     stores = [0]
 
     def store(q, pairs, reads):
         dma(q, pairs, "dst", 0, reads, [])
         stores[0] += 16 * len(pairs)
-    store("Y", [(T.li[0:1, 16 * k:16 * k + 16], T.lif[0:16, k:k + 1]) for k in range(6)], ["lif1"])
 
     mk = ["bt", "bm"]
     for c in range(3):
         pick_c("t1", 128 * c, 128, "big", HALF, 2 * HALF, "off1", 8 * c, mk + ["off1"], "t1c%d" % c)
         pick_s("t1", 128 * c, 128, "big", HALF, 2 * HALF, "off1", 8 * c, mk + ["off1"], "t1s%d" % c)
-        scores(c, "t1", "ur2", ["t1c%d" % c, "t1s%d" % c, "ur2", "ur2s"])
-    cp(T.off1f[:], T.off1[:], ["off1"], "off1f")
+        for f in (col, row):
+            f(c, "t1", "ur2", ["t1c%d" % c, "t1s%d" % c, "ur2", "ur2s"])
 
     def N(what, i, bank):
         if what == "D":
@@ -387,45 +419,53 @@ def rank_program(g, core, T, topo):
 
     def beside(c):
         if c == 0:
-            N("D", 0, 2), N("R", 0, 1), N("D", 1, 3)
-        elif c == 1:
-            N("R", 1, 5)
+            N("R", 0, 1), N("D", 0, 2), N("R", 1, 5), N("D", 1, 3)
         elif c == 2:
-            N("R", 2, 1), N("R", 3, 5), N("D", 2, 0)
-        else:
-            N("D", 3, 6)
-    order(beside)
+            N("R", 2, 1)
+        elif c == 3:
+            N("R", 3, 5), N("D", 2, 0), N("D", 3, 6)
+    cp(T.off1f[:], T.off1[:], ["off1"], "off1f")
+    cp(T.lif[:], T.lin[:], ["lin"], "lif")
+    store("Y", [(T.li[0:1, 16 * k:16 * k + 16], T.lif[0:16, k:k + 1]) for k in range(6)], ["lif"])
+    quant("big", CH, CH + 192, T.hx[:, 4 * CH:4 * CH + 768], hk("h0"), "bh0a")
+    order(beside, 0)
     add(0, 2, "hx", 0, CH, "hr1", "h1")
     add(1, 3, "hx", 0, CH, "hr1", "h1")
+    quant("big", CH + 192, HALF, T.hx[:, 4 * CH + 768:4 * HALF], hk("h0"), "bh0b")
     for t in range(3):
         V(lambda e, t=t: e.tensor_scalar(T.xo[:, t:96:4], T.thr[:, t:96:4], B(4, t, t + 1), float(HALF), OP.is_le, OP.mult),
           ["thr", "b4", "xoz", "xoq"], ["xo2%d" % t])
     quant("xoq", 0, 128, T.xo[:, 0:512], ["xoz"] + hk("xo2", 3), "xoq")
-    ycopy(2, 128, HALF - 128, ["bh0"])
-    mm(1, 128, "w2", 0, "xoq", 0, True, True, ["xoq", "w2"])
-    ycopy(3, HALF, CH, mk)
+    mm(7, 128, "w2", 0, "xoq", 0, True, True, ["xoq", "w2"])
     add(2, 0, "hx", 0, CH, "hr1", "h1")
     add(3, 6, "hx", 0, CH, "hr1", "h1")
-    quant("big", 0, 128, T.hx[:, 0:512], hk("h0") + hk("h1") + ["bh0"], "bh1")
-    ycopy(5, 0, 128, ["bh1"])
-    tt(T.off2f[:], T.off1f[:], B(1, 0, 24), OP.add, ["off1f", "b1"], "off2f")
+
+    def rowlist(t):
+        ts(T.wx[:, 48 + t:560:4], T.pm[:], B(4, t, t + 1), OP.is_equal, ["pm", "b4", "wxq"], "wx%d" % t)
+    rowlist(0), rowlist(1)
+    quant("big", 0, 128, T.hx[:, 0:512], hk("h0") + hk("h1") + ["bh0a"], "bh1")
+    tt(T.off2f[:], T.off1f[:], B(7, 0, 24), OP.add, ["off1f", "b7"], "off2f")
+    rowlist(2)
     cp(T.off2[:], T.off2f[:], ["off2f"], "off2")
-    al = ["bh0", "bh1", "off2"] + mk
-    yk = ["yw%d" % a for a in (0, 128, HALF, T0)]
+    al = ["bh0a", "bh0b", "bh1", "off2"] + mk
     for c in range(3):
         pick_c("oq", 128 * c, 128, "big", 0, 2 * HALF, "off2", 8 * c, al, "oq%d" % c)
-        store("Y", [(T.oc[:, 512 * c:512 * c + 512], u8("oq", 128 * c, 128 * c + 128))], ["oq%d" % c])
-    for a in (0, 192):
-        S(lambda e, a=a: e.activation(T.yb[:, a:a + 192], T.yw[:].indirect(T.off2[:, a // 16:a // 16 + 12]), AF.Copy),
-          yk + ["off2"], ["yb%d" % a])
-        store("Y", [(T.y[:, a:a + 192], T.yb[:, a:a + 192])], ["yb%d" % a])
-    pick_s("oq", 0, NT, "big", 0, 2 * HALF, "off2", 0, al, "oqs")
-    store("S", [(T.osc[4 * k:4 * k + 4, :], T.oqs[32 * k:32 * k + 4, :]) for k in range(4)], ["oqs"])
-    onehot()
-    list_mm(7)
-    cp(T.lif[:, 6:12], B(7, 0, 6), ["b7"], "lif2")
-    for q, ks in (("Y", (0, 1, 2)), ("S", (3, 4, 5))):
-        store(q, [(T.li[1:2, 16 * k:16 * k + 16], T.lif[0:16, 6 + k:7 + k]) for k in ks], ["lif2"])
+        pick_s("oq", 128 * c, 128, "big", 0, 2 * HALF, "off2", 8 * c, al, "oqs%d" % c)
+        mm((5, 6, 7)[c], 128, "wq", 0, "oq", 128 * c, True, True, ["wq", "oq%d" % c, "oqs%d" % c])
+        if c != 1:
+            a = max(128 * c - 128, 0)
+            store("Y", [(T.oc[:, 4 * a:512 * c + 512], u8("oq", a, 128 * c + 128))], ["oq1", "oq2"] if c else ["oq0"])
+    quant("wxq", 12, 140, T.wx[:, 48:560], ["wxz", "wx0", "wx1", "wx2"], "wxq")
+    for c in range(2):
+        act(T.yb[:, 128 * c:128 * c + 128], B(5 + c, 0, 128), AF.Copy, 0.0, 1.0, ["b%d" % (5 + c)], "yb%d" % c)
+    cp(T.yb[:, 256:384], B(7, 0, 128), ["b7"], "yb2")
+    mm(0, 128, "zq", 64, "wxq", 12, True, False, ["wxq", "zq"])
+    mm(0, 128, "zq", 62, "wxq", 12, False, True, ["wxq", "zq"])
+    store("Y", [(T.osc[4 * k:4 * k + 4, :], T.oqs[32 * k:32 * k + 4, :]) for k in range(4)], hk("oqs", 3))
+    for a, b in ((0, 1), (1, 3)):
+        store("Y", [(T.y[:, 128 * a:128 * b], T.yb[:, 128 * a:128 * b])], ["yb%d" % c for c in range(a, b)])
+    cp(T.lir[:], B(0, 0, 96), ["b0"], "lir")
+    store("S", [(T.li[1:2, :], T.lir[126:127, :])], ["lir"])
 
     for q in ("V", "T", "S", "G"):
         g.wait_ge(T.sem["s" + q], cnt[q])

@@ -7,6 +7,7 @@ CH = 96
 NT = 384
 HALF = CH + NT
 T0 = HALF + CH
+NZ = 226
 
 
 def sb(n, d):
@@ -23,35 +24,31 @@ def codes(**names):
 SCRATCH = {
     "ps": ("psum", [128, 4096], "float32"),
     "ub": sb(512, "bfloat16"), "xb": sb(4 * NT, "bfloat16"), "vb": sb(2048, "bfloat16"), "wb": sb(512, "bfloat16"),
-    "ones": sb(128, "bfloat16"), "zz": sb(560, "bfloat16"), "z16": sb(8, "uint16"), "eb": sb(520, "bfloat16"),
-    "zi": sb(256, "bfloat16"), "zj": sb(256, "bfloat16"),
+    "ones": sb(128, "bfloat16"), "z16": sb(8, "uint16"), "eb": sb(520, "bfloat16"), "urb": sb(512, "bfloat16"),
     "tri": sb(128, "bfloat16"), "q0": sb(128, "bfloat16"), "qm": sb(128, "bfloat16"), "pp": sb(128, "bfloat16"),
-    "pm": sb(128, "bfloat16"), "wa": sb(128, "bfloat16"),
-    "kc": sb(48, "float32"), "jj": sb(24, "int32"), "kk": sb(16, "int32"), "j16": sb(24, "int32"),
-    "ja": sb(24, "int32"), "jb": sb(24, "int32"), "jk": sb(16, "int32"), "g3": sb(16, "int32"), "g3a": sb(16, "int32"),
-    "g3b": sb(16, "int32"), "i3": sb(16, "int32"), "p16": sb(4, "int32"), "p128": sb(4, "int32"),
-    "p16f": sb(4, "float32"), "s4": sb(4, "float32"), "ab": sb(48, "float32"), "ab2": sb(8, "float32"),
-    "mk1": sb(16, "bfloat16"), "c88": sb(96, "float32"), "tha": sb(96, "float32"), "thr": sb(96, "float32"),
-    "w1b": sb(512, "bfloat16"), "w2b": sb(512, "bfloat16"), "zb": sb(768, "bfloat16"),
+    "pm": sb(128, "bfloat16"), "wa": sb(128, "bfloat16"), "kc": sb(48, "float32"), "jj": sb(24, "float32"),
+    "jx": sb(24, "float32"), "ab": sb(48, "float32"), "jbp": sb(1, "float32"), "ip": sb(1, "float32"),
+    "ip1": sb(1, "float32"), "ip2": sb(1, "float32"), "ip3": sb(1, "float32"), "p16f": sb(1, "float32"),
+    "c75": sb(1, "bfloat16"), "j96": sb(4, "float32"), "c88": sb(96, "float32"), "tha": sb(96, "float32"),
+    "thr": sb(96, "float32"), "w2b": sb(512, "bfloat16"), "zb": sb(4 * NZ, "bfloat16"),
     "sc": sb(3, "float32"), "dl": sb(3, "float32"), "mt": sb(NT, "float32"), "cmp": sb(4 * NT, "bfloat16"),
-    "kl": sb(52, "float32"), "x0": sb(48, "float32"), "wx": sb(560, "bfloat16"),
-    "sel": sb(8, "float32"), "rkp": sb(4, "float32"), "hl": sb(8, "float32"), "hm": sb(8, "float32"), "hn": sb(8, "float32"),
-    "xo": sb(544, "bfloat16"),
-    "lst1": sb(6, "uint16"), "offc": sb(3, "uint16"), "off2f": sb(24, "float32"), "off2": sb(24, "uint16"),
-    "lin": sb(6, "uint16"), "offd": ("dram", [128, 3], "uint16"), "off1": sb(24, "uint16"), "off1f": sb(24, "float32"),
+    "sg": sb(NT, "bfloat16"), "kl": sb(48, "float32"), "x0": sb(48, "float32"), "wx": sb(560, "bfloat16"),
+    "xo": sb(512, "bfloat16"), "ak": sb(4, "float32"), "offn": sb(3, "uint16"), "offs": ("dram", [128, 3], "uint16"),
+    "lst1": sb(6, "uint16"), "off2f": sb(24, "float32"), "off2": sb(24, "uint16"),
+    "lin": sb(6, "uint16"), "offd": ("dram", [128, 3], "uint16"), "off1a": sb(24, "uint16"), "off1": sb(24, "uint16"),
+    "off1f": sb(24, "float32"),
     "hrb": sb(4 * CH, "float32"), "hr0": sb(4 * NT, "float32"), "hr1": sb(4 * CH, "float32"),
     "hb": sb(512, "bfloat16"), "hx": sb(4 * HALF, "bfloat16"),
     "yb": sb(NT, "float32"), "lif": sb(6, "float32"), "lir": sb(96, "float32"),
 }
-SCRATCH.update(codes(uq=128, ur1=128, ur2=128, t0=NT, vq=512, wq=128, qe=CH + 512, w1=128, w2=128, zq=192, cq=NT, wxq=140,
-                     xoq=136, q1=CH, m1=128, big=2 * HALF, t1=NT, oq=NT))
-SCRATCH.update({"uin": sb(2, F8), "uins": sb(8, "uint8")})
-SEMAPHORES = ["sV", "sT", "sS", "sG", "du", "dx0", "dx1", "dx2", "dv0", "dv1", "dv2", "dv3", "dw", "doff", "dst",
-              "au", "aq", "at", "am", "al", "ao", "go", "ls"]
+SCRATCH.update(codes(uq=128, ur1=128, ur2=128, t0=NT, vq=512, wq=128, qe=CH + 512, w2=128, zq=NZ, cq=NT, wxq=140,
+                     xoq=128, q1=CH, m1=128, big=2 * HALF, t1=NT, oq=NT, uin=144))
+SEMAPHORES = ["sV", "sT", "sS", "sG", "du", "dx0", "dx1", "dx2", "dof", "dv0", "dv1", "dv2", "dv3", "dw", "doff", "dst",
+              "au", "aq", "at", "am", "al", "ao", "go", "go2", "ls"]
 
 OP = AluOpType
 AF = ActivationFunctionType
-BIG16 = 201326592.0
+BIG1, BIG16, BIG32 = 1.5 * 2.0 ** 23, 1.5 * 2.0 ** 27, 1.5 * 2.0 ** 28
 ULP = 1.03125 * 2.0 ** -24
 TINY = 1e-37
 C05 = 13421773 * 2.0 ** -28
@@ -132,13 +129,14 @@ def rank_program(g, core, T, topo):
     def u8(name, a, b):
         return T[name][:, a:b].bitcast(dt.uint8)
 
-    arrive("au", 8, ["uin", "uins"])
+    arrive("au", 8, ["uin"])
     arrive("aq", 32, ["qin"])
     arrive("at", 32, ["bt"])
     arrive("am", 32, ["bm"])
     arrive("al", 8, ["lin"])
     arrive("ao", 8, ["offd"])
     arrive("go", 1, ["go"])
+    arrive("go2", 1, ["go2"])
 
     def V(f, reads, writes):
         op("V", f, reads, writes)
@@ -152,8 +150,8 @@ def rank_program(g, core, T, topo):
     def memset(ap, c, key, after=()):
         V(lambda e: e.memset(ap, c), list(after), [key])
 
-    def iota(ap, pattern, key, cm=0):
-        G(lambda e: e.iota(ap, pattern, 0, cm, allow_small_or_imprecise_dtypes=True), [], [key])
+    def iota(ap, pattern, key, cm=0, base=0):
+        G(lambda e: e.iota(ap, pattern, base, cm, allow_small_or_imprecise_dtypes=True), [], [key])
 
     def ts(out, in0, s1, o, reads, key):
         V(lambda e: e.tensor_scalar(out, in0, s1, None, o), reads, [key])
@@ -168,7 +166,7 @@ def rank_program(g, core, T, topo):
         S(lambda e: e.activation(out, in_, f, bias=bias, scale=scale), reads, [key])
 
     def zero(out, w, key):
-        S(lambda e: e.activation(out, T.zz[:, 0:w], AF.Copy), ["zz"], [key])
+        S(lambda e: e.activation(out, T.ub[:, 8:8 + w], AF.Copy), ["ubz"], [key])
 
     def quant(out, a, b, src, reads, key):
         V(lambda e: e.quantize_mx(T[out][:, a:b], T[out + "s"][:, a:b], src), reads, [key])
@@ -196,115 +194,107 @@ def rank_program(g, core, T, topo):
         dma("Y", [(T.xb[:, 512 * c:512 * c + 512], T.x[:, 512 * c:512 * c + 512])], "dx%d" % c, 16, [], ["xb%d" % c])
 
     memset(T.ub[:, 8:512], 0.0, "ubz")
-    memset(T.zz[:], 0.0, "zz")
-    G(lambda e: e.iota(T.jj[:], [[0, 6], [128, 4]], 0, 1), [], ["jj"])
-    iota(T.zi[:], [[0, 16], [1, 4], [0, 4]], "zi")
     memset(T.ones[:], 1.0, "ones")
-    memset(T.eb[:], 0.0, "ebz")
-    memset(T.z16[:], 0, "z16")
+    iota(T.jj[:], [[0, 6], [128, 4]], "jj", 1)
+    iota(T.ip[:], [[0, 1]], "ip", 2)
+    G(lambda e: e.affine_select(T.c75[:], T.ub[:, 8:9], [[1, 1]], OP.not_equal, -7.5, 0, 1), ["ubz"], ["c75"])
+    iota(T.q0[:], [[0, 8], [1, 16]], "q0")
     quant("uq", 0, 128, T.ub[:], ["ub", "ubz"], "uq")
+    memset(T.zb[:], 0.0, "zbz")
+    memset(T.z16[:], 0, "z16")
+    quant("uin", 0, 128, T.zb[:, 0:512], ["zbz"], "uinz")
     wait("G", ["uq"], [])
     rid, pid, _ = topo.addr(prv)
     e0 = half(prv, 0)
     g.remote_dma_fused([RemoteDMATransfer(dst_ids=[DstId(rid=rid, pnc=pid)], dma_engine_mask=bits(e0[:4]), remote_sem=T.sem["au"],
-                                          src=u8("uq", 0, 2), dst=u8("uin", 0, 2)),
+                                          src=u8("uq", 0, 2), dst=u8("uin", 128, 130)),
                         RemoteDMATransfer(dst_ids=[DstId(rid=rid, pnc=pid)], dma_engine_mask=bits(e0[4:]), remote_sem=T.sem["au"],
-                                          src=T.uqs[:, 0:8], dst=T.uins[:, 0:8])], local_sem=T.sem["ls"])
+                                          src=T.uqs[:, 0:8], dst=T.uins[:, 128:136])], local_sem=T.sem["ls"])
     loc[0] += len(e0)
-    G(lambda e: e.affine_select(T.eb[:, 4:516:4], T.ones[:], [[-1, 128]], OP.is_equal, 0.0, 0, 1), ["ones", "ebz"], ["ebi"])
-    G(lambda e: e.iota(T.kk[:], [[1, 4], [0, 4]], 0, 0), [], ["kk"])
+    zero(T.eb[:, 0:504], 504, "ebz")
+    zero(T.eb[:, 504:520], 16, "ebz2")
+    G(lambda e: e.affine_select(T.eb[:, 4:516:4], T.ones[:], [[-1, 128]], OP.is_equal, 0.0, 0, 1), ["ones", "ebz", "ebz2"], ["ebi"])
     G(lambda e: e.affine_select(T.tri[:], T.ones[:], [[1, 128]], OP.is_gt, 0.0, 0, -1), ["ones"], ["tri"])
-    iota(T.q0[:], [[0, 8], [1, 16]], "q0")
+    iota(T.kc[:], [[0, 2], [16, 6], [0, 4]], "kc")
     iota(T.pp[:], [[1, 128]], "pp")
-    zero(T.wx[:], 560, "wxz")
-    act(T.zb[:, 0:256], T.zi[:], AF.Relu, 1.0, -1.0, ["zi"], "zb0")
-    act(T.zj[:], T.zi[:], AF.Abs, -1.0, 1.0, ["zi"], "zj")
-    zero(T.zb[:, 512:768], 256, "zb2")
-    act(T.zb[:, 256:512], T.zj[:], AF.Relu, 1.0, -1.0, ["zj"], "zb1")
-    ts(T.j16[:], T.jj[:], 16, OP.add, ["jj"], "j16")
-    ts(T.jk[:], T.jj[:, 0:16], 4, OP.logical_shift_right, ["jj"], "jk")
-    ts(T.p16[:], T.jj[:, 0:4], 15, OP.bitwise_and, ["jj"], "p16")
-    ts(T.ja[:], T.j16[:], 480, OP.bitwise_and, ["j16"], "ja")
-    ts(T.g3a[:], T.jk[:], 11, OP.mult, ["jk"], "g3a")
-    ts(T.p128[:], T.p16[:], 8, OP.mult, ["p16"], "p128")
-    tt(T.jb[:], T.jj[:], T.ja[:], OP.subtract, ["jj", "ja"], "jb")
-    ts(T.g3[:], T.g3a[:], 5, OP.logical_shift_right, ["g3a"], "g3")
-    cp(T.ab[:, 0:24], T.ja[:], ["ja"], "aba")
-    cp(T.ab[:, 24:48], T.jb[:], ["jb"], "abb")
-    cp(T.p16f[:], T.p16[:], ["p16"], "p16f")
-    tt(T.s4[:], T.p128[:], T.g3[:, 0:4], OP.add, ["p128", "g3"], "s4")
+    iota(T.j96[:], [[128, 4]], "j96", 1, CH)
+    act(T.jx[:], T.jj[:], AF.Identity, BIG32, 1.0, ["jj"], "jx")
+    act(T.ip1[:], T.ip[:], AF.Identity, -15.0, 1.0, ["ip"], "ip1")
+    act(T.ab[:, 0:24], T.jx[:], AF.Identity, -BIG32, 1.0, ["jx"], "aba")
+    act(T.ip2[:], T.ip1[:], AF.Identity, BIG1, 1.0 / 32, ["ip1"], "ip2")
+    act(T.jbp[:], T.ab[:, 0:1], AF.Identity, T.jj[:, 0:1], -1.0, ["aba", "jj"], "jbp")
+    act(T.ip3[:], T.ip2[:], AF.Identity, -BIG1, 1.0, ["ip2"], "ip3")
+    act(T.ab[:, 24:48], T.ub[:, 8:32], AF.Identity, T.jbp[:, 0:1], 1.0, ["ubz", "jbp"], "abb")
+    act(T.cmp[:, 3:4 * NT:4], T.ub[:, 8:8 + NT], AF.Identity, T.c75[:, 0:1], 1.0, ["ubz", "c75"], "cmk")
+    act(T.p16f[:], T.ip3[:], AF.Identity, T.jj[:, 0:1], -16.0, ["ip3", "jj"], "p16f")
+    zero(T.wx[:, 51:560:4], 128, "wxz")
+    act(T.qm[:], T.q0[:], AF.Identity, -7.5, 1.0, ["q0"], "qm")
+    for t in range(4):
+        for a in range(2):
+            k = 24 if t < 3 else 12
+            act(T.zb[:, 388 * a + 8 + t:388 * a + 8 + 16 * k:16], T.ones[:, 0:k], AF.Copy, 0.0, 1.0, ["ones", "zbz", "uinz"], "zo%d%d" % (a, t))
+    act(T.zb[:, 888:891], T.ub[:, 8:11], AF.Identity, T.jbp[:, 0:1], 1.0, ["ubz", "jbp", "zbz"], "zba")
+    act(T.zb[:, 896:899], T.ab[:, 0:3], AF.Copy, 0.0, 1.0, ["aba", "zbz"], "zbb")
+
+    def EQ(b):
+        quant("qe", CH + 128 * b, CH + 128 * b + 128, T.eb[:, 4 - b:516 - b], ["ebz", "ebz2", "ebi"], "eq%d" % b)
     for c in range(3):
         quant("t0", 128 * c, 128 * c + 128, T.xb[:, 512 * c:512 * c + 512], ["xb%d" % c], "t0%d" % c)
         if c < 2:
-            for b in (2 * c, 2 * c + 1):
-                quant("qe", CH + 128 * b, CH + 128 * b + 128, T.eb[:, 4 - b:516 - b], ["ebz", "ebi"], "eq%d" % b)
+            EQ(c)
     t0 = hk("t0", 3)
     send(nx2, u8("big", T0, T0 + NT), u8("t0", 0, NT), "at", topo.engines(core, nx2), t0)
     send(nx2, T.bigs[:, T0:T0 + NT], T.t0s[:, 0:NT], "at", topo.engines(core, nx2), [])
     g.sem_inc(T.sem["go"], 1)
     for i in range(4):
         dma("Y", [(T.vb[:, 512 * i:512 * i + 512], T.v[:, 512 * i:512 * i + 512])], "dv%d" % i, 16, ["go", "uin"], ["vb%d" % i])
-    for c in range(3):
-        G(lambda e, c=c: e.affine_select(T.cmp[:, 512 * c + c:512 * c + 512:4], T.zz[:, 0:128], [[0, 128]], OP.not_equal, -7.5, 0, 1),
-          ["zz"], ["cm%d%d" % (c, c)])
-    iota(T.kc[:], [[0, 2], [16, 6], [0, 4]], "kc")
-    cp(T.zb[:, 752:755], T.jb[:, 0:3], ["jb", "zb2"], "zba")
-    cp(T.zb[:, 760:763], T.ja[:, 0:3], ["ja", "zb2"], "zbb")
-    memset(T.ab[:, 3:48:4], 0.0, "ab", ["aba", "abb"])
-    quant("zq", 0, 192, T.zb[:], hk("zb", 3) + ["zba", "zbb"], "zq")
-    pick_c("ur1", 0, 128, "uin", 0, 2, "z16", 0, ["uin", "uins", "z16"], "ur1")
-    pick_s("ur1", 0, 128, "uin", 0, 2, "z16", 0, ["uin", "uins", "z16"], "ur1s")
-    for t in range(4):
-        ts(T.w1b[:, t:512:4], T.pp[:], T.s4[:, t:t + 1], OP.is_equal, ["pp", "s4"], "w1b%d" % t)
-    ts(T.g3b[:], T.g3[:], 3, OP.mult, ["g3"], "g3b")
-    ts(T.ab2[:, 0:4], T.ja[:, 0:4], float(CH), OP.add, ["ja"], "ab2a")
-    act(T.qm[:], T.q0[:], AF.Identity, -7.5, 1.0, ["q0"], "qm")
-    act(T.wa[:], T.q0[:], AF.Abs, T.p16f[:, 0:1], -1.0, ["q0", "p16f"], "wa")
-    for t in range(2):
-        act(T.w2b[:, t:512:4], T.wa[:], AF.Relu, 1.0, -1.0, ["wa"], "w2b%d" % t)
 
     ROW = (0, 6, 7)
+    SC = 126
 
-    def col(c, tok, ur, keys):
-        mm(1 + c, 128, tok, 128 * c, ur, 0, True, True, keys)
+    def col(c, tok, ur, keys, at=0):
+        mm(1 + c, 128, tok, 128 * c, ur, at, True, True, keys)
 
     def row(c, tok, ur, keys):
         mm(ROW[c], 128, ur, 0, tok, 128 * c, True, True, keys)
 
-    def order(beside, early):
-        def against(c, t):
-            ts(T.cmp[:, 512 * c + t:512 * c + 512:4], B(ROW[c], 0, 128), B(1 + t, 0, 1), OP.is_le if t < c else OP.is_lt,
-               ["b%d" % ROW[c], "b%d" % (1 + t)], "cm%d%d" % (c, t))
-        against(0, 1)
-        if not early:
-            against(1, 0)
-        cp(T.sc[:], ps[:, 512:2048:512], ["b1", "b2", "b3"], "sc")
-        act(T.dl[:], T.sc[:], AF.Abs, TINY, ULP, ["sc"], "dl")
-        for c, t in ((0, 2),) + ((1, 0),) * early + ((1, 2), (2, 0), (2, 1)):
-            against(c, t)
-        for c in range(3):
-            act(T.mt[:, 128 * c:128 * c + 128], T.tri[:], AF.Identity, T.sc[:, c:c + 1], T.dl[:, c:c + 1],
-                ["tri", "sc", "dl"], "mt%d" % c)
+    def slot(c, t):
+        return T.cmp[:, 512 * c + t:512 * c + 512:4]
 
-        def diagonal(c):
-            tt(T.cmp[:, 512 * c + 3:512 * c + 512:4], B(ROW[c], 0, 128), T.mt[:, 128 * c:128 * c + 128], OP.is_lt,
-               ["b%d" % ROW[c], "mt%d" % c], "cm%d3" % c)
-
-        def pack(c):
-            quant("cq", 128 * c, 128 * c + 128, T.cmp[:, 512 * c:512 * c + 512], hk("cm%d" % c), "cq%d" % c)
-            beside(c)
-        diagonal(0), diagonal(1), pack(0), diagonal(2), pack(1), pack(2)
-        for c in range(3):
-            mm(4, 128, "cq", 128 * c, "zq", (0, 64, 2)[c], c == 0, c == 2, ["cq%d" % c, "zq"])
-        beside(3)
-
-    def R(i, bank, q, q0, w, out, w2, keys, by="S"):
-        mm(bank, w, "vq", 128 * i, q, q0, True, True, keys + ["vq%d" % i])
-        o = T[out][:, w2 * i:w2 * i + w2]
-        if by == "S":
-            S(lambda e: e.activation(o, B(bank, 0, w2), AF.Relu, scale=0.05), ["b%d" % bank], [out + str(i)])
+    def against(c, t):
+        if c == t:
+            tt(slot(c, c), B(ROW[c], 0, 128), T.mt[:, 128 * c:128 * c + 128], OP.is_lt, ["b%d" % ROW[c], "mt%d" % c], "cm%d%d" % (c, c))
         else:
-            V(lambda e: e.tensor_scalar(o, B(bank, 0, w2), 0.0, C05, OP.max, OP.mult), ["b%d" % bank], [out + str(i)])
+            ts(slot(c, t), B(ROW[c], 0, 128), T.sc[:, t:t + 1], OP.is_le if t < c else OP.is_lt, ["b%d" % ROW[c], "sc%d" % t], "cm%d%d" % (c, t))
+
+    def sign(c, t):
+        k = c + t - 1
+        act(T.sg[:, 128 * k:128 * k + 128], B(ROW[c], 0, 128), AF.Sign, T.sc[:, t:t + 1], -1.0, ["b%d" % ROW[c], "sc%d" % t], "sg%d" % k)
+
+    def relu(c, t):
+        k = c + t - 1
+        act(slot(c, t), T.sg[:, 128 * k:128 * k + 128], AF.Relu, 0.0, 1.0, ["sg%d" % k], "cm%d%d" % (c, t))
+
+    def score(a, b):
+        S(lambda e: e.activation(T.sc[:, a:b], ps[:, 512 * a + 512 + SC:512 * b + 512:512], AF.Copy),
+          ["b%d" % (1 + c) for c in range(a, b)], ["sc%d" % c for c in range(a, b)])
+
+    def step(a, b):
+        S(lambda e: e.activation(T.dl[:, a:b], ps[:, 512 * a + 512 + SC:512 * b + 512:512], AF.Abs, bias=TINY, scale=ULP),
+          ["b%d" % (1 + c) for c in range(a, b)], ["dl%d" % c for c in range(a, b)])
+
+    def shift(c):
+        act(T.mt[:, 128 * c:128 * c + 128], T.tri[:], AF.Identity, T.sc[:, c:c + 1], T.dl[:, c:c + 1], ["tri", "sc%d" % c, "dl%d" % c], "mt%d" % c)
+
+    def pack(c):
+        quant("cq", 128 * c, 128 * c + 128, T.cmp[:, 512 * c:512 * c + 512], hk("cm%d" % c, 3) + ["cmk"], "cq%d" % c)
+
+    def position(c):
+        mm(4, 128, "cq", 128 * c, "zq", (2, 98, 0)[c], c == 2, c == 0, ["cq%d" % c, "zq"])
+
+    def R(i, bank, q, q0, w, out, w2, keys):
+        mm(bank, w, "vq", 128 * i, q, q0, True, True, keys + ["vq%d" % i])
+        act(T[out][:, w2 * i:w2 * i + w2], B(bank, 0, w2), AF.Relu, 0.0, C05, ["b%d" % bank], out + str(i))
 
     def D(i, bank, q, q0, w, keys):
         mm(bank, w, "qe", CH + 128 * i, q, q0, True, True, keys + ["eq%d" % i])
@@ -324,80 +314,89 @@ def rank_program(g, core, T, topo):
     def VQ(i):
         quant("vq", 128 * i, 128 * i + 128, T.vb[:, 512 * i:512 * i + 512], ["vb%d" % i], "vq%d" % i)
 
-    for f, c in ((row, 0), (col, 1), (col, 0), (col, 2), (row, 1), (row, 2)):
-        f(c, "t0", "ur1", ["t0%d" % c, "ur1", "ur1s"])
-    order(lambda c: None, 1)
-    zero(T.xo[:], 544, "xoz")
-    for t in range(2, 4):
-        act(T.w2b[:, t:512:4], T.wa[:], AF.Relu, 1.0, -1.0, ["wa"], "w2b%d" % t)
-    quant("w1", 0, 128, T.w1b[:], hk("w1b"), "w1")
-    tt(T.i3[:], T.jk[:], T.g3b[:], OP.subtract, ["jk", "g3b"], "i3")
-    cp(T.ab2[:, 4:8], T.jb[:, 0:4], ["jb"], "ab2b")
-    V(lambda e: e.tensor_scalar(T.kl[:, 0:48], B(4, 0, 48), BIG16, BIG16, OP.add, OP.subtract), ["b4"], ["kl"])
-    ts(T.sel[:], B(4, 0, 8), CH - 7.5, OP.is_lt, ["b4"], "sel")
-    tt(T.x0[:], T.kl[:, 0:48], T.kc[:], OP.is_equal, ["kl", "kc"], "x0")
+    uk = ["uin", "uinz"]
+    EQ(2)
+    for c in range(3):
+        col(c, "t0", "uin", ["t0%d" % c] + uk, 2)
+    pick_s("ur1", 0, 128, "uin", 128, 130, "z16", 0, uk + ["z16"], "ur1s")
+    pick_c("ur1", 0, 128, "uin", 128, 130, "z16", 0, uk + ["z16"], "ur1")
+    for c in (2, 0, 1):
+        row(c, "t0", "ur1", ["t0%d" % c, "ur1", "ur1s"])
+    quant("zq", 0, NZ, T.zb[:], ["zbz", "zba", "zbb"] + hk("zo0") + hk("zo1"), "zq")
+    score(0, 3), step(0, 3), shift(2), sign(0, 2), sign(1, 2), shift(1), shift(0), relu(1, 2), relu(0, 2)
+    for c, t in ((2, 0), (2, 1), (2, 2), (0, 1), (1, 0), (1, 1)):
+        against(c, t)
+    pack(2), against(0, 0), pack(1), pack(0)
+    position(2), position(1), position(0)
+    D0(0)
+    for t in range(4):
+        act(T.urb[:, t:512:4], T.ub[:, 8:136], AF.Identity, T.ub[:, t:t + 1], 1.0, ["ub", "ubz"], "urb%d" % t)
+    act(T.wa[:], T.q0[:], AF.Abs, T.p16f[:, 0:1], -1.0, ["q0", "p16f"], "wa")
+    act(T.c88[:, 0:48], T.ones[:, 0:48], AF.Identity, CH - 9.0, 1.0, ["ones"], "c88a")
+    act(T.c88[:, 48:96], T.ones[:, 0:48], AF.Identity, CH - 1.5, 1.0, ["ones"], "c88b")
+    zero(T.hb[:, 4 * CH:512], 128, "hbz")
+    zero(T.xo[:, 96:512], 416, "xoz")
+    V(lambda e: e.tensor_scalar(T.kl[:], B(4, 0, 48), BIG16, BIG16, OP.add, OP.subtract), ["b4"], ["kl"])
+    V(lambda e: e.tensor_scalar(T.ak[:], B(4, 48, 52), CH - 0.5, 1000.0, OP.subtract, OP.mult), ["b4"], ["ak"])
+
+    def offn(t):
+        V(lambda e: e.tensor_scalar(T.offn[:, t:t + 1], B(4, 48 + t, 49 + t), T.ak[:, t:t + 1], T.j96[:, t:t + 1], OP.max, OP.min),
+          ["b4", "ak", "j96"], ["offn%d" % t])
+    tt(T.x0[:], T.kl[:], T.kc[:], OP.is_equal, ["kl", "kc"], "x0")
     for t in range(3):
         V(lambda e, t=t: e.tensor_scalar(T.wx[:, 48 + t:560:4], T.qm[:], T.kl[:, t:t + 1], B(4, t, t + 1), OP.add, OP.is_equal),
-          ["kl", "qm", "b4", "wxz"], ["wx%d" % t])
+          ["kl", "qm", "b4"], ["wx%d" % t])
         if t == 1:
-            tt(T.wx[:, 0:48], T.x0[:], T.ab[:], OP.mult, ["x0", "ab", "wxz"], "wxx")
-    ts(T.rkp[:], B(4, 0, 4), 7.5, OP.add, ["b4"], "rkp")
+            tt(T.wx[:, 0:48], T.x0[:], T.ab[:], OP.mult, ["x0", "aba", "abb"], "wxx")
+    offn(0)
     quant("wxq", 0, 140, T.wx[:], ["wxz", "wx0", "wx1", "wx2", "wxx"], "wxq")
     mm(5, 128, "wxq", 12, "wxq", 0, True, False, ["wxq"])
     mm(5, 128, "wxq", 12, "wxq", 6, False, True, ["wxq"])
-    tt(T.mk1[:], T.i3[:], T.kk[:], OP.is_equal, ["i3", "kk"], "mk1a")
-    tt(T.kl[:, 48:52], T.rkp[:], T.kl[:, 44:48], OP.subtract, ["rkp", "kl"], "kl2")
-    memset(T.mk1[:, 3:16:4], 0.0, "mk1", ["mk1a"])
+    D0(1)
+    offn(1), offn(2), EQ(3)
+    dma("Y", [(T.offs[k:128:8, :], T.offn[16 * k:16 * k + 16, :]) for k in range(8)], "dof", 128, hk("offn", 3), ["offs"])
+    dma("Y", [(T.wb[:], T.w[:])], "dw", 16, ["go2"], ["wb"])
     cp(T.lst1[:], B(5, 0, 6), ["b5"], "lst1")
-    tt(T.hl[:], T.kl[:, 44:52], T.ab2[:], OP.subtract, ["kl", "kl2", "ab2a", "ab2b"], "hl")
-    pick_c("q1", 0, CH, "t0", 0, NT, "lst1", 0, t0 + ["lst1"], "q1")
     pick_s("q1", 0, CH, "t0", 0, NT, "lst1", 0, t0 + ["lst1"], "q1s")
+    pick_c("q1", 0, CH, "t0", 0, NT, "lst1", 0, t0 + ["lst1"], "q1")
     send(nxt, u8("qe", 0, CH), u8("q1", 0, CH), "aq", topo.engines(core, nxt), ["q1"])
     send(nxt, T.qes[:, 0:CH], T.q1s[:, 0:CH], "aq", topo.engines(core, nxt), ["q1s"])
-    tt(T.hm[:], T.hl[:], T.sel[:], OP.mult, ["hl", "sel"], "hm")
-    quant("w2", 0, 128, T.w2b[:], hk("w2b"), "w2")
-    tt(T.hn[:], T.hm[:], T.ab2[:], OP.add, ["hm", "ab2a", "ab2b"], "hn")
-    for k in range(2):
-        for t in range(3):
-            ts(T.xo[:, 16 * k + t:16 * k + 16:4], T.mk1[:, t:16:4], T.hn[:, 4 * k + t:4 * k + t + 1], OP.mult,
-               ["hn", "mk1", "xoz"], "xo%d%d" % (k, t))
-    quant("xoq", 0, 136, T.xo[:], ["xoz"] + hk("xo0", 3) + hk("xo1", 3), "xoq")
-    act(T.c88[:], T.ones[:, 0:96], AF.Identity, CH - 7.5, 0.0, ["ones"], "c88")
-    act(T.pm[:], T.pp[:], AF.Identity, -7.5, 1.0, ["pp"], "pm")
-    zero(T.hb[:, 4 * CH:512], 128, "hbz")
-    pick_s("ur2", 0, 128, "uq", 0, 2, "z16", 0, ["uq", "z16"], "ur2s")
-    G(lambda e: e.affine_select(T.tha[:], T.c88[:], [[-16, 24], [128, 4]], OP.is_ge, CH + 392.5, 0, 1), ["c88"], ["tha"])
-    G(lambda e: e.affine_select(T.thr[:], T.tha[:], [[16, 24], [-128, 4]], OP.is_ge, CH + 392.5, 15, -1), ["tha"], ["thr"])
-    D0(0), D0(1), D0(2)
-    mm(6, 128, "w1", 0, "xoq", 0, True, False, ["xoq", "w1"])
-    mm(6, 128, "w1", 0, "xoq", 4, False, True, ["xoq", "w1"])
-    VQ(0), VQ(1)
-    cp(T.offc[:], B(6, 0, 3), ["b6"], "offc")
-    send(nx2, T.offd[:], T.offc[:], "ao", half(nx2, 0), ["offc"])
+    g.sem_inc(T.sem["go2"], 1)
     send(nx2, T.lin[:], T.lst1[:], "al", half(nx2, 0), ["lst1"])
-    VQ(2), VQ(3)
-    pick_c("ur2", 0, 128, "uq", 0, 2, "z16", 0, ["uq", "z16"], "ur2")
-    R0(0, 7)
+    send(nx2, T.offd[:], T.offs[:], "ao", half(nx2, 0), ["offs"])
+    VQ(0), VQ(1), VQ(2), VQ(3)
+    for t in range(4):
+        act(T.w2b[:, t:512:4], T.wa[:], AF.Relu, float(HALF), -float(HALF), ["wa"], "w2b%d" % t)
+    R0(0, 7), R0(1, 6), R0(2, 2)
+    quant("ur2", 0, 128, T.urb[:], hk("urb"), "ur2")
+    quant("w2", 0, 128, T.w2b[:], hk("w2b"), "w2")
+    A0(0)
+    G(lambda e: e.affine_select(T.tha[:], T.c88[:], [[-16, 24], [128, 4]], OP.is_ge, CH + 392.5, 0, 1), ["c88a", "c88b"], ["tha"])
+    G(lambda e: e.affine_select(T.thr[:], T.tha[:], [[16, 24], [-128, 4]], OP.is_ge, CH + 392.5, 15, -1), ["tha"], ["thr"])
 
-    def RB(i, bank, by):
-        R(i, bank, "qe", 0, 128, "hrb", CH, ["qin", "eq0"], by)
+    def RB(i, bank):
+        R(i, bank, "qe", 0, 128, "hrb", CH, ["qin", "eq0"])
 
     def DB(i, bank):
         D(i, bank, "qe", 0, 128, ["qin", "eq0"])
 
     def AB(i, bank):
         add(i, bank, "hb", 0, CH, "hrb", "hb")
-    RB(0, 4, "V"), RB(1, 5, "S"), RB(2, 3, "V"), DB(0, 6), RB(3, 4, "S"), DB(2, 7), DB(1, 5), DB(3, 3)
-    AB(0, 6), AB(2, 7), AB(1, 5), AB(3, 3)
+    A0(1)
+    RB(0, 4), RB(1, 5), RB(2, 3), RB(3, 6), DB(0, 7), DB(1, 4), DB(2, 5), DB(3, 3)
+    AB(0, 7), AB(1, 4), AB(2, 5), AB(3, 3)
     quant("m1", 0, 128, T.hb[:], ["hbz"] + hk("hb"), "m1")
     send(nxt, u8("big", HALF, HALF + CH), u8("m1", 0, CH), "am", topo.engines(core, nxt), ["m1"])
     send(nxt, T.bigs[:, HALF:HALF + CH], T.m1s[:, 0:CH], "am", topo.engines(core, nxt), [])
-    dma("Y", [(T.wb[:], T.w[:])], "dw", 16, ["qin"], ["wb"])
-    dma("Y", [(T.off1[16 * h:16 * h + 16, :], T.offd[:]) for h in range(8)], "doff", 128, ["offd"], ["off1"])
-    R0(1, 4), R0(2, 6), D0(3), R0(3, 7)
-    for i in range(4):
-        A0(i)
+    dma("Y", [(T.off1a[16 * h:16 * h + 16, :], T.offd[:]) for h in range(8)], "doff", 128, ["offd"], ["off1a"])
+    R0(3, 6), D0(2), D0(3)
+    act(T.pm[:], T.pp[:], AF.Identity, -7.5, 1.0, ["pp"], "pm")
     quant("wq", 0, 128, T.wb[:], ["wb"], "wq")
+    A0(2)
+    A0(3)
+    quant("big", CH + 192, HALF, T.hx[:, 4 * CH + 768:4 * HALF], hk("h0"), "bh0b")
+    for t in range(3):
+        cp(T.off1[:, 8 * t:8 * t + 8], T.off1a[:, t:24:3], ["off1a"], "off1%d" % t)
     stores = [0]
 
     def store(q, pairs, reads):
@@ -406,10 +405,10 @@ def rank_program(g, core, T, topo):
 
     mk = ["bt", "bm"]
     for c in range(3):
-        pick_c("t1", 128 * c, 128, "big", HALF, 2 * HALF, "off1", 8 * c, mk + ["off1"], "t1c%d" % c)
-        pick_s("t1", 128 * c, 128, "big", HALF, 2 * HALF, "off1", 8 * c, mk + ["off1"], "t1s%d" % c)
+        pick_s("t1", 128 * c, 128, "big", HALF, 2 * HALF, "off1", 8 * c, mk + ["off1%d" % c], "t1s%d" % c)
+        pick_c("t1", 128 * c, 128, "big", HALF, 2 * HALF, "off1", 8 * c, mk + ["off1%d" % c], "t1c%d" % c)
         for f in (col, row):
-            f(c, "t1", "ur2", ["t1c%d" % c, "t1s%d" % c, "ur2", "ur2s"])
+            f(c, "t1", "ur2", ["t1c%d" % c, "t1s%d" % c, "ur2"])
 
     def N(what, i, bank):
         if what == "D":
@@ -417,54 +416,53 @@ def rank_program(g, core, T, topo):
         else:
             R(i, bank, "big", HALF, 128, "hr1", CH, mk)
 
-    def beside(c):
-        if c == 0:
-            N("R", 0, 1), N("D", 0, 2), N("R", 1, 5), N("D", 1, 3)
-        elif c == 2:
-            N("R", 2, 1)
-        elif c == 3:
-            N("R", 3, 5), N("D", 2, 0), N("D", 3, 6)
-    cp(T.off1f[:], T.off1[:], ["off1"], "off1f")
-    cp(T.lif[:], T.lin[:], ["lin"], "lif")
-    store("Y", [(T.li[0:1, 16 * k:16 * k + 16], T.lif[0:16, k:k + 1]) for k in range(6)], ["lif"])
+    score(0, 2), step(0, 2), score(2, 3), step(2, 3), shift(0)
+    cp(T.off1f[:], T.off1[:], hk("off1", 3), "off1f")
+    against(0, 1), against(1, 0)
+    sign(1, 2), shift(2)
+    against(2, 0), against(2, 1), against(0, 0)
+    sign(0, 2), shift(1), relu(1, 2), relu(0, 2)
     quant("big", CH, CH + 192, T.hx[:, 4 * CH:4 * CH + 768], hk("h0"), "bh0a")
-    order(beside, 0)
+    against(2, 2), against(1, 1), pack(2)
+    cp(T.lif[:], T.lin[:], ["lin"], "lif")
+    pack(1), pack(0)
+    store("Y", [(T.li[0:1, 16 * k:16 * k + 16], T.lif[0:16, k:k + 1]) for k in range(6)], ["lif"])
+    N("R", 0, 1), N("D", 0, 2), N("R", 1, 5), N("D", 1, 3)
+    N("R", 2, 7), position(2), N("R", 3, 6), position(1), position(0), N("D", 2, 1), N("D", 3, 5)
     add(0, 2, "hx", 0, CH, "hr1", "h1")
     add(1, 3, "hx", 0, CH, "hr1", "h1")
-    quant("big", CH + 192, HALF, T.hx[:, 4 * CH + 768:4 * HALF], hk("h0"), "bh0b")
-    for t in range(3):
-        V(lambda e, t=t: e.tensor_scalar(T.xo[:, t:96:4], T.thr[:, t:96:4], B(4, t, t + 1), float(HALF), OP.is_le, OP.mult),
-          ["thr", "b4", "xoz", "xoq"], ["xo2%d" % t])
-    quant("xoq", 0, 128, T.xo[:, 0:512], ["xoz"] + hk("xo2", 3), "xoq")
-    mm(7, 128, "w2", 0, "xoq", 0, True, True, ["xoq", "w2"])
-    add(2, 0, "hx", 0, CH, "hr1", "h1")
-    add(3, 6, "hx", 0, CH, "hr1", "h1")
+    tt(T.xo[:, 0:96], T.thr[:], B(4, 0, 96), OP.is_le, ["thr", "b4"], "xo")
 
     def rowlist(t):
         ts(T.wx[:, 48 + t:560:4], T.pm[:], B(4, t, t + 1), OP.is_equal, ["pm", "b4", "wxq"], "wx%d" % t)
-    rowlist(0), rowlist(1)
+    rowlist(0)
+    quant("xoq", 0, 128, T.xo[:], ["xoz", "xo"], "xoq")
+    mm(7, 128, "w2", 0, "xoq", 0, True, True, ["xoq", "w2"])
+    add(2, 1, "hx", 0, CH, "hr1", "h1")
+    add(3, 5, "hx", 0, CH, "hr1", "h1")
+    rowlist(1)
     quant("big", 0, 128, T.hx[:, 0:512], hk("h0") + hk("h1") + ["bh0a"], "bh1")
     tt(T.off2f[:], T.off1f[:], B(7, 0, 24), OP.add, ["off1f", "b7"], "off2f")
     rowlist(2)
     cp(T.off2[:], T.off2f[:], ["off2f"], "off2")
+    quant("wxq", 12, 140, T.wx[:, 48:560], ["wxz", "wx0", "wx1", "wx2"], "wxq")
+    mm(0, 128, "zq", 98, "wxq", 12, True, False, ["wxq", "zq"])
+    mm(0, 128, "zq", 96, "wxq", 12, False, True, ["wxq", "zq"])
     al = ["bh0a", "bh0b", "bh1", "off2"] + mk
     for c in range(3):
-        pick_c("oq", 128 * c, 128, "big", 0, 2 * HALF, "off2", 8 * c, al, "oq%d" % c)
         pick_s("oq", 128 * c, 128, "big", 0, 2 * HALF, "off2", 8 * c, al, "oqs%d" % c)
+        pick_c("oq", 128 * c, 128, "big", 0, 2 * HALF, "off2", 8 * c, al, "oq%d" % c)
         mm((5, 6, 7)[c], 128, "wq", 0, "oq", 128 * c, True, True, ["wq", "oq%d" % c, "oqs%d" % c])
         if c != 1:
             a = max(128 * c - 128, 0)
             store("Y", [(T.oc[:, 4 * a:512 * c + 512], u8("oq", a, 128 * c + 128))], ["oq1", "oq2"] if c else ["oq0"])
-    quant("wxq", 12, 140, T.wx[:, 48:560], ["wxz", "wx0", "wx1", "wx2"], "wxq")
     for c in range(2):
         act(T.yb[:, 128 * c:128 * c + 128], B(5 + c, 0, 128), AF.Copy, 0.0, 1.0, ["b%d" % (5 + c)], "yb%d" % c)
-    cp(T.yb[:, 256:384], B(7, 0, 128), ["b7"], "yb2")
-    mm(0, 128, "zq", 64, "wxq", 12, True, False, ["wxq", "zq"])
-    mm(0, 128, "zq", 62, "wxq", 12, False, True, ["wxq", "zq"])
-    store("Y", [(T.osc[4 * k:4 * k + 4, :], T.oqs[32 * k:32 * k + 4, :]) for k in range(4)], hk("oqs", 3))
-    for a, b in ((0, 1), (1, 3)):
-        store("Y", [(T.y[:, 128 * a:128 * b], T.yb[:, 128 * a:128 * b])], ["yb%d" % c for c in range(a, b)])
     cp(T.lir[:], B(0, 0, 96), ["b0"], "lir")
+    cp(T.yb[:, 256:384], B(7, 0, 128), ["b7"], "yb2")
+    store("Y", [(T.osc[4 * k:4 * k + 4, :], T.oqs[32 * k:32 * k + 4, :]) for k in range(4)], hk("oqs", 3))
+    for a, b in ((0, 2), (2, 3)):
+        store("Y", [(T.y[:, 128 * a:128 * b], T.yb[:, 128 * a:128 * b])], ["yb%d" % c for c in range(a, b)])
     store("S", [(T.li[1:2, :], T.lir[126:127, :])], ["lir"])
 
     for q in ("V", "T", "S", "G"):

import numpy as np
from concourse.bass import DstId, RemoteDMATransfer
from concourse.mybir import dt, AluOpType, AxisListType, ActivationFunctionType

F8 = "float8_e4m3fn_x4"
CH = 96
NT = 384
HALF = CH + NT
T0 = HALF + CH
NZ = 226


def sb(n, d):
    return ("sbuf", [128, n], d)


def codes(**names):
    d = {}
    for k, n in names.items():
        d[k], d[k + "s"] = sb(n, F8), sb(n, "uint8")
    return d


SCRATCH = {
    "ps": ("psum", [128, 4096], "float32"),
    "ub": sb(512, "bfloat16"), "xb": sb(4 * NT, "bfloat16"), "vb": sb(2048, "bfloat16"), "wb": sb(512, "bfloat16"),
    "ones": sb(128, "bfloat16"), "z16": sb(8, "uint16"), "eb": sb(520, "bfloat16"), "urb": sb(512, "bfloat16"),
    "tri": sb(128, "bfloat16"), "q0": sb(128, "bfloat16"), "qm": sb(128, "bfloat16"), "pp": sb(128, "bfloat16"),
    "pm": sb(128, "bfloat16"), "wa": sb(128, "bfloat16"), "kc": sb(48, "float32"), "jj": sb(24, "float32"),
    "jx": sb(24, "float32"), "ab": sb(48, "float32"), "jbp": sb(1, "float32"), "ip": sb(1, "float32"),
    "ip1": sb(1, "float32"), "ip2": sb(1, "float32"), "ip3": sb(1, "float32"), "p16f": sb(1, "float32"),
    "c75": sb(1, "bfloat16"), "j96": sb(4, "float32"), "c88": sb(96, "float32"), "tha": sb(96, "float32"),
    "thr": sb(96, "float32"), "w2b": sb(512, "bfloat16"), "zb": sb(4 * NZ, "bfloat16"),
    "sc": sb(3, "float32"), "dl": sb(3, "float32"), "mt": sb(NT, "float32"), "cmp": sb(4 * NT, "bfloat16"),
    "sg": sb(NT, "bfloat16"), "kl": sb(48, "float32"), "x0": sb(48, "float32"), "wx": sb(560, "bfloat16"),
    "xo": sb(512, "bfloat16"), "ak": sb(4, "float32"), "offn": sb(3, "uint16"), "offs": ("dram", [128, 3], "uint16"),
    "lst1": sb(6, "uint16"), "off2f": sb(24, "float32"), "off2": sb(24, "uint16"),
    "lin": sb(6, "uint16"), "offd": ("dram", [128, 3], "uint16"), "off1a": sb(24, "uint16"), "off1": sb(24, "uint16"),
    "off1f": sb(24, "float32"),
    "hrb": sb(4 * CH, "float32"), "hr0": sb(4 * NT, "float32"), "hr1": sb(4 * CH, "float32"),
    "hb": sb(512, "bfloat16"), "hx": sb(4 * HALF, "bfloat16"),
    "yb": sb(NT, "float32"), "lif": sb(6, "float32"), "lir": sb(96, "float32"),
}
SCRATCH.update(codes(uq=128, ur1=128, ur2=128, t0=NT, vq=512, wq=128, qe=CH + 512, w2=128, zq=NZ, cq=NT, wxq=140,
                     xoq=128, q1=CH, m1=128, big=2 * HALF, t1=NT, oq=NT, uin=144))
SEMAPHORES = ["sV", "sT", "sS", "sG", "du", "dx0", "dx1", "dx2", "dof", "dv0", "dv1", "dv2", "dv3", "dw", "doff", "dst",
              "au", "aq", "at", "am", "al", "ao", "go", "go2", "ls"]

OP = AluOpType
AF = ActivationFunctionType
BIG1, BIG16, BIG32 = 1.5 * 2.0 ** 23, 1.5 * 2.0 ** 27, 1.5 * 2.0 ** 28
ULP = 1.03125 * 2.0 ** -24
TINY = 1e-37
C05 = 13421773 * 2.0 ** -28
BANKS = ["b%d" % k for k in range(8)]


def sched(g, T):
    eng = {"V": g.vector, "T": g.tensor, "S": g.scalar, "G": g, "Y": g.sync}
    cnt = {"V": 0, "T": 0, "S": 0, "G": 0}
    wr, rd, seen = {}, {}, {}

    def wait(q, reads, writes):
        req = {}
        for k in reads:
            for qq, s, v in wr.get(k, []):
                req[s] = max(req.get(s, 0), v)
            if k in BANKS:
                for qq, s, v in rd.get(k, []):
                    if qq != q:
                        req[s] = max(req.get(s, 0), v)
        for k in writes:
            for qq, s, v in wr.get(k, []) + rd.get(k, []):
                if qq != q or q != "T":
                    req[s] = max(req.get(s, 0), v)
        for s, v in req.items():
            if seen.get((q, s), 0) < v:
                eng[q].wait_ge(T.sem[s], v)
                seen[(q, s)] = v

    def note(q, s, v, reads, writes):
        for k in reads:
            rd.setdefault(k, []).append((q, s, v))
        for k in writes:
            wr[k] = [(q, s, v)]
            rd[k] = []

    def op(q, call, reads, writes):
        wait(q, reads, writes)
        cnt[q] += 1
        call(eng[q]).then_inc(T.sem["s" + q], 1)
        note(q, "s" + q, cnt[q], reads, writes)

    def dma(q, pairs, s, v, reads, writes):
        wait(q, reads, writes)
        for o, i in pairs:
            eng[q].dma_start(o, i).then_inc(T.sem[s], 16)
        note("dma", s, v, reads, writes)

    def arrive(s, v, keys):
        for k in keys:
            wr[k] = [("far", s, v)]
    return op, dma, arrive, wait, cnt


def rank_program(g, core, T, topo):
    r = T.rank_of(core)
    if r is None:
        return
    n = len(T.cores)
    nxt, nx2, prv = T.cores[(r + 1) % n], T.cores[(r + 2) % n], T.cores[(r - 1) % n]
    op, dma, arrive, wait, cnt = sched(g, T)
    ps = T.ps
    loc = [0]

    def half(dst, k):
        e = topo.engines(core, dst)
        return e[:len(e) // 2] if k == 0 else e[len(e) // 2:]

    def bits(es):
        return sum(1 << e for e in es)

    def send(dst, out, src, sem, es, reads):
        wait("G", reads, [])
        rid, pid, _ = topo.addr(dst)
        g.remote_dma(out, src, T.sem[sem], T.sem["ls"], pid, rid, bits(es))
        loc[0] += len(es)

    def u8(name, a, b):
        return T[name][:, a:b].bitcast(dt.uint8)

    arrive("au", 8, ["uin"])
    arrive("aq", 32, ["qin"])
    arrive("at", 32, ["bt"])
    arrive("am", 32, ["bm"])
    arrive("al", 8, ["lin"])
    arrive("ao", 8, ["offd"])
    arrive("go", 1, ["go"])
    arrive("go2", 1, ["go2"])

    def V(f, reads, writes):
        op("V", f, reads, writes)

    def S(f, reads, writes):
        op("S", f, reads, writes)

    def G(f, reads, writes):
        op("G", f, reads, writes)

    def memset(ap, c, key, after=()):
        V(lambda e: e.memset(ap, c), list(after), [key])

    def iota(ap, pattern, key, cm=0, base=0):
        G(lambda e: e.iota(ap, pattern, base, cm, allow_small_or_imprecise_dtypes=True), [], [key])

    def ts(out, in0, s1, o, reads, key):
        V(lambda e: e.tensor_scalar(out, in0, s1, None, o), reads, [key])

    def tt(out, in0, in1, o, reads, key):
        V(lambda e: e.tensor_tensor(out, in0, in1, o), reads, [key])

    def cp(out, in_, reads, key):
        V(lambda e: e.tensor_copy(out, in_), reads, [key])

    def act(out, in_, f, bias, scale, reads, key):
        S(lambda e: e.activation(out, in_, f, bias=bias, scale=scale), reads, [key])

    def zero(out, w, key):
        S(lambda e: e.activation(out, T.ub[:, 8:8 + w], AF.Copy), ["ubz"], [key])

    def quant(out, a, b, src, reads, key):
        V(lambda e: e.quantize_mx(T[out][:, a:b], T[out + "s"][:, a:b], src), reads, [key])

    def mm(bank, w, L, l0, R, r0, start, stop, reads):
        op("T", lambda e: e.matmul_mx(ps[:, 512 * bank:512 * bank + w], T[L][:, l0:l0 + 128], T[L + "s"][:, l0:l0 + 128],
                                      T[R][:, r0:r0 + w], T[R + "s"][:, r0:r0 + w], start, stop), reads, ["b%d" % bank])

    def B(bank, a, b):
        return ps[:, 512 * bank + a:512 * bank + b]

    def pick_c(dst, d0, w, src, a, b, off, o0, reads, key):
        V(lambda e: e.tensor_copy(T[dst][:, d0:d0 + w].bitcast(dt.uint32),
                                  T[src][:, a:b].bitcast(dt.uint32).indirect(T[off][:, o0:o0 + w // 16])), reads, [key])

    def pick_s(dst, d0, w, src, a, b, off, o0, reads, key):
        S(lambda e: e.activation(T[dst + "s"][:, d0:d0 + w], T[src + "s"][:, a:b].indirect(T[off][:, o0:o0 + w // 16]),
                                 AF.Copy), reads, [key])

    def hk(key, k=4):
        return [key + str(i) for i in range(k)]

    dma("Y", [(T.ub[:, 0:8], T.u[:, 0:8])], "du", 16, [], ["ub"])
    for c in range(3):
        dma("Y", [(T.xb[:, 512 * c:512 * c + 512], T.x[:, 512 * c:512 * c + 512])], "dx%d" % c, 16, [], ["xb%d" % c])

    memset(T.ub[:, 8:512], 0.0, "ubz")
    memset(T.ones[:], 1.0, "ones")
    iota(T.jj[:], [[0, 6], [128, 4]], "jj", 1)
    iota(T.ip[:], [[0, 1]], "ip", 2)
    G(lambda e: e.affine_select(T.c75[:], T.ub[:, 8:9], [[1, 1]], OP.not_equal, -7.5, 0, 1), ["ubz"], ["c75"])
    iota(T.q0[:], [[0, 8], [1, 16]], "q0")
    quant("uq", 0, 128, T.ub[:], ["ub", "ubz"], "uq")
    memset(T.zb[:], 0.0, "zbz")
    memset(T.z16[:], 0, "z16")
    quant("uin", 0, 128, T.zb[:, 0:512], ["zbz"], "uinz")
    wait("G", ["uq"], [])
    rid, pid, _ = topo.addr(prv)
    e0 = half(prv, 0)
    g.remote_dma_fused([RemoteDMATransfer(dst_ids=[DstId(rid=rid, pnc=pid)], dma_engine_mask=bits(e0[:4]), remote_sem=T.sem["au"],
                                          src=u8("uq", 0, 2), dst=u8("uin", 128, 130)),
                        RemoteDMATransfer(dst_ids=[DstId(rid=rid, pnc=pid)], dma_engine_mask=bits(e0[4:]), remote_sem=T.sem["au"],
                                          src=T.uqs[:, 0:8], dst=T.uins[:, 128:136])], local_sem=T.sem["ls"])
    loc[0] += len(e0)
    zero(T.eb[:, 0:504], 504, "ebz")
    zero(T.eb[:, 504:520], 16, "ebz2")
    G(lambda e: e.affine_select(T.eb[:, 4:516:4], T.ones[:], [[-1, 128]], OP.is_equal, 0.0, 0, 1), ["ones", "ebz", "ebz2"], ["ebi"])
    G(lambda e: e.affine_select(T.tri[:], T.ones[:], [[1, 128]], OP.is_gt, 0.0, 0, -1), ["ones"], ["tri"])
    iota(T.kc[:], [[0, 2], [16, 6], [0, 4]], "kc")
    iota(T.pp[:], [[1, 128]], "pp")
    iota(T.j96[:], [[128, 4]], "j96", 1, CH)
    act(T.jx[:], T.jj[:], AF.Identity, BIG32, 1.0, ["jj"], "jx")
    act(T.ip1[:], T.ip[:], AF.Identity, -15.0, 1.0, ["ip"], "ip1")
    act(T.ab[:, 0:24], T.jx[:], AF.Identity, -BIG32, 1.0, ["jx"], "aba")
    act(T.ip2[:], T.ip1[:], AF.Identity, BIG1, 1.0 / 32, ["ip1"], "ip2")
    act(T.jbp[:], T.ab[:, 0:1], AF.Identity, T.jj[:, 0:1], -1.0, ["aba", "jj"], "jbp")
    act(T.ip3[:], T.ip2[:], AF.Identity, -BIG1, 1.0, ["ip2"], "ip3")
    act(T.ab[:, 24:48], T.ub[:, 8:32], AF.Identity, T.jbp[:, 0:1], 1.0, ["ubz", "jbp"], "abb")
    act(T.cmp[:, 3:4 * NT:4], T.ub[:, 8:8 + NT], AF.Identity, T.c75[:, 0:1], 1.0, ["ubz", "c75"], "cmk")
    act(T.p16f[:], T.ip3[:], AF.Identity, T.jj[:, 0:1], -16.0, ["ip3", "jj"], "p16f")
    zero(T.wx[:, 51:560:4], 128, "wxz")
    act(T.qm[:], T.q0[:], AF.Identity, -7.5, 1.0, ["q0"], "qm")
    for t in range(4):
        for a in range(2):
            k = 24 if t < 3 else 12
            act(T.zb[:, 388 * a + 8 + t:388 * a + 8 + 16 * k:16], T.ones[:, 0:k], AF.Copy, 0.0, 1.0, ["ones", "zbz", "uinz"], "zo%d%d" % (a, t))
    act(T.zb[:, 888:891], T.ub[:, 8:11], AF.Identity, T.jbp[:, 0:1], 1.0, ["ubz", "jbp", "zbz"], "zba")
    act(T.zb[:, 896:899], T.ab[:, 0:3], AF.Copy, 0.0, 1.0, ["aba", "zbz"], "zbb")

    def EQ(b):
        quant("qe", CH + 128 * b, CH + 128 * b + 128, T.eb[:, 4 - b:516 - b], ["ebz", "ebz2", "ebi"], "eq%d" % b)
    for c in range(3):
        quant("t0", 128 * c, 128 * c + 128, T.xb[:, 512 * c:512 * c + 512], ["xb%d" % c], "t0%d" % c)
        if c < 2:
            EQ(c)
    t0 = hk("t0", 3)
    send(nx2, u8("big", T0, T0 + NT), u8("t0", 0, NT), "at", topo.engines(core, nx2), t0)
    send(nx2, T.bigs[:, T0:T0 + NT], T.t0s[:, 0:NT], "at", topo.engines(core, nx2), [])
    g.sem_inc(T.sem["go"], 1)
    for i in range(4):
        dma("Y", [(T.vb[:, 512 * i:512 * i + 512], T.v[:, 512 * i:512 * i + 512])], "dv%d" % i, 16, ["go", "uin"], ["vb%d" % i])

    ROW = (0, 6, 7)
    SC = 126

    def col(c, tok, ur, keys, at=0):
        mm(1 + c, 128, tok, 128 * c, ur, at, True, True, keys)

    def row(c, tok, ur, keys):
        mm(ROW[c], 128, ur, 0, tok, 128 * c, True, True, keys)

    def slot(c, t):
        return T.cmp[:, 512 * c + t:512 * c + 512:4]

    def against(c, t):
        if c == t:
            tt(slot(c, c), B(ROW[c], 0, 128), T.mt[:, 128 * c:128 * c + 128], OP.is_lt, ["b%d" % ROW[c], "mt%d" % c], "cm%d%d" % (c, c))
        else:
            ts(slot(c, t), B(ROW[c], 0, 128), T.sc[:, t:t + 1], OP.is_le if t < c else OP.is_lt, ["b%d" % ROW[c], "sc%d" % t], "cm%d%d" % (c, t))

    def sign(c, t):
        k = c + t - 1
        act(T.sg[:, 128 * k:128 * k + 128], B(ROW[c], 0, 128), AF.Sign, T.sc[:, t:t + 1], -1.0, ["b%d" % ROW[c], "sc%d" % t], "sg%d" % k)

    def relu(c, t):
        k = c + t - 1
        act(slot(c, t), T.sg[:, 128 * k:128 * k + 128], AF.Relu, 0.0, 1.0, ["sg%d" % k], "cm%d%d" % (c, t))

    def score(a, b):
        S(lambda e: e.activation(T.sc[:, a:b], ps[:, 512 * a + 512 + SC:512 * b + 512:512], AF.Copy),
          ["b%d" % (1 + c) for c in range(a, b)], ["sc%d" % c for c in range(a, b)])

    def step(a, b):
        S(lambda e: e.activation(T.dl[:, a:b], ps[:, 512 * a + 512 + SC:512 * b + 512:512], AF.Abs, bias=TINY, scale=ULP),
          ["b%d" % (1 + c) for c in range(a, b)], ["dl%d" % c for c in range(a, b)])

    def shift(c):
        act(T.mt[:, 128 * c:128 * c + 128], T.tri[:], AF.Identity, T.sc[:, c:c + 1], T.dl[:, c:c + 1], ["tri", "sc%d" % c, "dl%d" % c], "mt%d" % c)

    def pack(c):
        quant("cq", 128 * c, 128 * c + 128, T.cmp[:, 512 * c:512 * c + 512], hk("cm%d" % c, 3) + ["cmk"], "cq%d" % c)

    def position(c):
        mm(4, 128, "cq", 128 * c, "zq", (2, 98, 0)[c], c == 2, c == 0, ["cq%d" % c, "zq"])

    def R(i, bank, q, q0, w, out, w2, keys):
        mm(bank, w, "vq", 128 * i, q, q0, True, True, keys + ["vq%d" % i])
        act(T[out][:, w2 * i:w2 * i + w2], B(bank, 0, w2), AF.Relu, 0.0, C05, ["b%d" % bank], out + str(i))

    def D(i, bank, q, q0, w, keys):
        mm(bank, w, "qe", CH + 128 * i, q, q0, True, True, keys + ["eq%d" % i])

    def add(i, bank, h, c0, w, hr, key):
        tt(T[h][:, 4 * c0 + i:4 * (c0 + w):4], T[hr][:, w * i:w * i + w], B(bank, 0, w), OP.add, [hr + str(i), "b%d" % bank], key + str(i))

    def D0(b):
        D(b, b, "big", T0, NT, ["bt"])

    def R0(i, bank):
        R(i, bank, "big", T0, NT, "hr0", NT, ["bt"])

    def A0(i):
        add(i, i, "hx", CH, NT, "hr0", "h0")

    def VQ(i):
        quant("vq", 128 * i, 128 * i + 128, T.vb[:, 512 * i:512 * i + 512], ["vb%d" % i], "vq%d" % i)

    uk = ["uin", "uinz"]
    EQ(2)
    for c in range(3):
        col(c, "t0", "uin", ["t0%d" % c] + uk, 2)
    pick_s("ur1", 0, 128, "uin", 128, 130, "z16", 0, uk + ["z16"], "ur1s")
    pick_c("ur1", 0, 128, "uin", 128, 130, "z16", 0, uk + ["z16"], "ur1")
    for c in (2, 0, 1):
        row(c, "t0", "ur1", ["t0%d" % c, "ur1", "ur1s"])
    quant("zq", 0, NZ, T.zb[:], ["zbz", "zba", "zbb"] + hk("zo0") + hk("zo1"), "zq")
    score(0, 3), step(0, 3), shift(2), sign(0, 2), sign(1, 2), shift(1), shift(0), relu(1, 2), relu(0, 2)
    for c, t in ((2, 0), (2, 1), (2, 2), (0, 1), (1, 0), (1, 1)):
        against(c, t)
    pack(2), against(0, 0), pack(1), pack(0)
    position(2), position(1), position(0)
    D0(0)
    for t in range(4):
        act(T.urb[:, t:512:4], T.ub[:, 8:136], AF.Identity, T.ub[:, t:t + 1], 1.0, ["ub", "ubz"], "urb%d" % t)
    act(T.wa[:], T.q0[:], AF.Abs, T.p16f[:, 0:1], -1.0, ["q0", "p16f"], "wa")
    act(T.c88[:, 0:48], T.ones[:, 0:48], AF.Identity, CH - 9.0, 1.0, ["ones"], "c88a")
    act(T.c88[:, 48:96], T.ones[:, 0:48], AF.Identity, CH - 1.5, 1.0, ["ones"], "c88b")
    zero(T.hb[:, 4 * CH:512], 128, "hbz")
    zero(T.xo[:, 96:512], 416, "xoz")
    V(lambda e: e.tensor_scalar(T.kl[:], B(4, 0, 48), BIG16, BIG16, OP.add, OP.subtract), ["b4"], ["kl"])
    V(lambda e: e.tensor_scalar(T.ak[:], B(4, 48, 52), CH - 0.5, 1000.0, OP.subtract, OP.mult), ["b4"], ["ak"])

    def offn(t):
        V(lambda e: e.tensor_scalar(T.offn[:, t:t + 1], B(4, 48 + t, 49 + t), T.ak[:, t:t + 1], T.j96[:, t:t + 1], OP.max, OP.min),
          ["b4", "ak", "j96"], ["offn%d" % t])
    tt(T.x0[:], T.kl[:], T.kc[:], OP.is_equal, ["kl", "kc"], "x0")
    for t in range(3):
        V(lambda e, t=t: e.tensor_scalar(T.wx[:, 48 + t:560:4], T.qm[:], T.kl[:, t:t + 1], B(4, t, t + 1), OP.add, OP.is_equal),
          ["kl", "qm", "b4"], ["wx%d" % t])
        if t == 1:
            tt(T.wx[:, 0:48], T.x0[:], T.ab[:], OP.mult, ["x0", "aba", "abb"], "wxx")
    offn(0)
    quant("wxq", 0, 140, T.wx[:], ["wxz", "wx0", "wx1", "wx2", "wxx"], "wxq")
    mm(5, 128, "wxq", 12, "wxq", 0, True, False, ["wxq"])
    mm(5, 128, "wxq", 12, "wxq", 6, False, True, ["wxq"])
    D0(1)
    offn(1), offn(2), EQ(3)
    dma("Y", [(T.offs[k:128:8, :], T.offn[16 * k:16 * k + 16, :]) for k in range(8)], "dof", 128, hk("offn", 3), ["offs"])
    dma("Y", [(T.wb[:], T.w[:])], "dw", 16, ["go2"], ["wb"])
    cp(T.lst1[:], B(5, 0, 6), ["b5"], "lst1")
    pick_s("q1", 0, CH, "t0", 0, NT, "lst1", 0, t0 + ["lst1"], "q1s")
    pick_c("q1", 0, CH, "t0", 0, NT, "lst1", 0, t0 + ["lst1"], "q1")
    send(nxt, u8("qe", 0, CH), u8("q1", 0, CH), "aq", topo.engines(core, nxt), ["q1"])
    send(nxt, T.qes[:, 0:CH], T.q1s[:, 0:CH], "aq", topo.engines(core, nxt), ["q1s"])
    g.sem_inc(T.sem["go2"], 1)
    send(nx2, T.lin[:], T.lst1[:], "al", half(nx2, 0), ["lst1"])
    send(nx2, T.offd[:], T.offs[:], "ao", half(nx2, 0), ["offs"])
    VQ(0), VQ(1), VQ(2), VQ(3)
    for t in range(4):
        act(T.w2b[:, t:512:4], T.wa[:], AF.Relu, float(HALF), -float(HALF), ["wa"], "w2b%d" % t)
    R0(0, 7), R0(1, 6), R0(2, 2)
    quant("ur2", 0, 128, T.urb[:], hk("urb"), "ur2")
    quant("w2", 0, 128, T.w2b[:], hk("w2b"), "w2")
    A0(0)
    G(lambda e: e.affine_select(T.tha[:], T.c88[:], [[-16, 24], [128, 4]], OP.is_ge, CH + 392.5, 0, 1), ["c88a", "c88b"], ["tha"])
    G(lambda e: e.affine_select(T.thr[:], T.tha[:], [[16, 24], [-128, 4]], OP.is_ge, CH + 392.5, 15, -1), ["tha"], ["thr"])

    def RB(i, bank):
        R(i, bank, "qe", 0, 128, "hrb", CH, ["qin", "eq0"])

    def DB(i, bank):
        D(i, bank, "qe", 0, 128, ["qin", "eq0"])

    def AB(i, bank):
        add(i, bank, "hb", 0, CH, "hrb", "hb")
    A0(1)
    RB(0, 4), RB(1, 5), RB(2, 3), RB(3, 6), DB(0, 7), DB(1, 4), DB(2, 5), DB(3, 3)
    AB(0, 7), AB(1, 4), AB(2, 5), AB(3, 3)
    quant("m1", 0, 128, T.hb[:], ["hbz"] + hk("hb"), "m1")
    send(nxt, u8("big", HALF, HALF + CH), u8("m1", 0, CH), "am", topo.engines(core, nxt), ["m1"])
    send(nxt, T.bigs[:, HALF:HALF + CH], T.m1s[:, 0:CH], "am", topo.engines(core, nxt), [])
    dma("Y", [(T.off1a[16 * h:16 * h + 16, :], T.offd[:]) for h in range(8)], "doff", 128, ["offd"], ["off1a"])
    R0(3, 6), D0(2), D0(3)
    act(T.pm[:], T.pp[:], AF.Identity, -7.5, 1.0, ["pp"], "pm")
    quant("wq", 0, 128, T.wb[:], ["wb"], "wq")
    A0(2)
    A0(3)
    quant("big", CH + 192, HALF, T.hx[:, 4 * CH + 768:4 * HALF], hk("h0"), "bh0b")
    for t in range(3):
        cp(T.off1[:, 8 * t:8 * t + 8], T.off1a[:, t:24:3], ["off1a"], "off1%d" % t)
    stores = [0]

    def store(q, pairs, reads):
        dma(q, pairs, "dst", 0, reads, [])
        stores[0] += 16 * len(pairs)

    mk = ["bt", "bm"]
    for c in range(3):
        pick_s("t1", 128 * c, 128, "big", HALF, 2 * HALF, "off1", 8 * c, mk + ["off1%d" % c], "t1s%d" % c)
        pick_c("t1", 128 * c, 128, "big", HALF, 2 * HALF, "off1", 8 * c, mk + ["off1%d" % c], "t1c%d" % c)
        for f in (col, row):
            f(c, "t1", "ur2", ["t1c%d" % c, "t1s%d" % c, "ur2"])

    def N(what, i, bank):
        if what == "D":
            D(i, bank, "big", HALF, 128, mk)
        else:
            R(i, bank, "big", HALF, 128, "hr1", CH, mk)

    score(0, 2), step(0, 2), score(2, 3), step(2, 3), shift(0)
    cp(T.off1f[:], T.off1[:], hk("off1", 3), "off1f")
    against(0, 1), against(1, 0)
    sign(1, 2), shift(2)
    against(2, 0), against(2, 1), against(0, 0)
    sign(0, 2), shift(1), relu(1, 2), relu(0, 2)
    quant("big", CH, CH + 192, T.hx[:, 4 * CH:4 * CH + 768], hk("h0"), "bh0a")
    against(2, 2), against(1, 1), pack(2)
    cp(T.lif[:], T.lin[:], ["lin"], "lif")
    pack(1), pack(0)
    store("Y", [(T.li[0:1, 16 * k:16 * k + 16], T.lif[0:16, k:k + 1]) for k in range(6)], ["lif"])
    N("R", 0, 1), N("D", 0, 2), N("R", 1, 5), N("D", 1, 3)
    N("R", 2, 7), position(2), N("R", 3, 6), position(1), position(0), N("D", 2, 1), N("D", 3, 5)
    add(0, 2, "hx", 0, CH, "hr1", "h1")
    add(1, 3, "hx", 0, CH, "hr1", "h1")
    tt(T.xo[:, 0:96], T.thr[:], B(4, 0, 96), OP.is_le, ["thr", "b4"], "xo")

    def rowlist(t):
        ts(T.wx[:, 48 + t:560:4], T.pm[:], B(4, t, t + 1), OP.is_equal, ["pm", "b4", "wxq"], "wx%d" % t)
    rowlist(0)
    quant("xoq", 0, 128, T.xo[:], ["xoz", "xo"], "xoq")
    mm(7, 128, "w2", 0, "xoq", 0, True, True, ["xoq", "w2"])
    add(2, 1, "hx", 0, CH, "hr1", "h1")
    add(3, 5, "hx", 0, CH, "hr1", "h1")
    rowlist(1)
    quant("big", 0, 128, T.hx[:, 0:512], hk("h0") + hk("h1") + ["bh0a"], "bh1")
    tt(T.off2f[:], T.off1f[:], B(7, 0, 24), OP.add, ["off1f", "b7"], "off2f")
    rowlist(2)
    cp(T.off2[:], T.off2f[:], ["off2f"], "off2")
    quant("wxq", 12, 140, T.wx[:, 48:560], ["wxz", "wx0", "wx1", "wx2"], "wxq")
    mm(0, 128, "zq", 98, "wxq", 12, True, False, ["wxq", "zq"])
    mm(0, 128, "zq", 96, "wxq", 12, False, True, ["wxq", "zq"])
    al = ["bh0a", "bh0b", "bh1", "off2"] + mk
    for c in range(3):
        pick_s("oq", 128 * c, 128, "big", 0, 2 * HALF, "off2", 8 * c, al, "oqs%d" % c)
        pick_c("oq", 128 * c, 128, "big", 0, 2 * HALF, "off2", 8 * c, al, "oq%d" % c)
        mm((5, 6, 7)[c], 128, "wq", 0, "oq", 128 * c, True, True, ["wq", "oq%d" % c, "oqs%d" % c])
        if c != 1:
            a = max(128 * c - 128, 0)
            store("Y", [(T.oc[:, 4 * a:512 * c + 512], u8("oq", a, 128 * c + 128))], ["oq1", "oq2"] if c else ["oq0"])
    for c in range(2):
        act(T.yb[:, 128 * c:128 * c + 128], B(5 + c, 0, 128), AF.Copy, 0.0, 1.0, ["b%d" % (5 + c)], "yb%d" % c)
    cp(T.lir[:], B(0, 0, 96), ["b0"], "lir")
    cp(T.yb[:, 256:384], B(7, 0, 128), ["b7"], "yb2")
    store("Y", [(T.osc[4 * k:4 * k + 4, :], T.oqs[32 * k:32 * k + 4, :]) for k in range(4)], hk("oqs", 3))
    for a, b in ((0, 2), (2, 3)):
        store("Y", [(T.y[:, 128 * a:128 * b], T.yb[:, 128 * a:128 * b])], ["yb%d" % c for c in range(a, b)])
    store("S", [(T.li[1:2, :], T.lir[126:127, :])], ["lir"])

    for q in ("V", "T", "S", "G"):
        g.wait_ge(T.sem["s" + q], cnt[q])
    g.wait_ge(T.sem["ls"], loc[0])
    g.wait_ge(T.sem["dst"], stores[0])
